import numpy as np
import ml_dtypes


def mxq(x, axis, fmt="e4m3"):
    dtype, down = {"e4m3": (ml_dtypes.float8_e4m3fn, 7), "e5m2": (ml_dtypes.float8_e5m2, 14)}[fmt]
    v = np.moveaxis(np.asarray(x, np.float32).astype(ml_dtypes.bfloat16).astype(np.float64), axis, -1)
    blocks = v.reshape(v.shape[:-1] + (-1, 32))
    amax = np.abs(blocks).max(-1, keepdims=True)
    byte = np.maximum(np.where(amax > 0, np.frexp(amax)[1] - 1 + 127, 0) - down, 1)
    scale = np.exp2(byte - 127.0)
    codes = (blocks / scale).astype(np.float32).astype(dtype).astype(np.float64)
    return np.moveaxis((codes * scale).reshape(v.shape), -1, axis)


WIDE = False


def mx_kscale(k):
    if not WIDE:
        return np.ones(k)
    levels = np.array([10, -10, 5, -5, 0])
    if k % 512:
        return np.exp2(np.random.permutation(np.resize(levels, k // 32))).repeat(32)
    a = np.empty((k // 512, 16))
    for p in range(k // 512):
        a[p, :8] = np.random.permutation(np.resize(levels, 8))
        for g in range(8):
            far = levels[np.abs(levels - a[p, g]) >= 10]
            a[p, g + 8] = far[np.random.randint(len(far))]
    return np.exp2(a.ravel()).repeat(32)


def f64(x):
    return np.asarray(x).astype(np.float64)


def striped(idx):
    return np.tile(idx.reshape(-1, 16).T, (8, 1)).astype(np.uint16)


def unstriped(offs):
    return offs[:16].T.reshape(-1).astype(np.int64)


E2M1 = np.array([0.0, 0.5, 1.0, 1.5, 2.0, 3.0, 4.0, 6.0, -0.0, -0.5, -1.0, -1.5, -2.0, -3.0, -4.0, -6.0])


def pack_weight(w, fmt):
    k, n = w.shape
    w = f64(np.asarray(w, np.float32).astype(ml_dtypes.bfloat16)).reshape(k // 32, 32, n)
    amax = np.abs(w).max(1)
    if fmt == "e4m3":
        byte = np.frexp(amax)[1] - 1 + 127 - 7
    else:
        mant, ex = np.frexp(amax / 6.0)
        byte = np.where(mant > 0.5, ex, ex - 1) + 127
    byte = np.clip(np.where(amax > 0, byte, 1), 1, 254)
    scaled = (w * np.exp2(127.0 - byte)[:, None, :]).reshape(k, n).astype(np.float32)
    by_word = np.ascontiguousarray(scaled.reshape(k // 512, 128, 4, n).transpose(0, 1, 3, 2))
    if fmt == "e4m3":
        words = by_word.astype(ml_dtypes.float8_e4m3fn).view(np.uint8)
    else:
        c = by_word.astype(ml_dtypes.float4_e2m1fn).view(np.uint8) & 0xF
        words = (c[..., 0::2] | (c[..., 1::2] << 4)).reshape(k // 512, 128, 2 * n)
    return np.ascontiguousarray(words), np.ascontiguousarray(byte.astype(np.uint8).reshape(k // 512, 16, n))


def unpack_weight(words, scales, fmt):
    g, _, n = scales.shape
    words = np.ascontiguousarray(words).reshape(g, 128, n, -1)
    if fmt == "e4m3":
        vals = words.view(ml_dtypes.float8_e4m3fn).astype(np.float64)
    else:
        nib = np.empty((g, 128, n, 4), np.uint8)
        nib[..., 0::2] = words & 0xF
        nib[..., 1::2] = words >> 4
        vals = E2M1[nib]
    vals = vals * np.repeat(np.exp2(scales.astype(np.float64) - 127.0), 8, axis=1)[..., None]
    return vals.transpose(0, 1, 3, 2).reshape(g * 512, n)


def gelu(v):
    return 0.5 * v * (1.0 + np.tanh(np.sqrt(2.0 / np.pi) * (v + 0.044715 * v**3)))


def striped8(idx):
    return np.concatenate([v.reshape(-1, 16).T for v in idx]).astype(np.uint16)


def unstriped8(offs):
    return np.stack([offs[16 * g:16 * g + 16].T.reshape(-1) for g in range(8)]).astype(np.int64)


def heads(h, wgt, idx8):
    r = np.arange(h.shape[0])
    return wgt[r // 4 % 128] * h[r[:, None], idx8[r % 512 // 64]]


def put_heads(h, wgs, idx8, t2):
    r = np.arange(h.shape[0])
    page = np.zeros((h.shape[0], t2))
    page[r[:, None], idx8[r % 512 // 64]] = wgs[r // 4 % 128] * h
    return page


K, T, S, H, T2, P, N = 512, 4096, 1024, 1024, 2048, 1024, 384

def setup_inputs():
    n = np.random.standard_normal
    s = mx_kscale(K)[:, None]
    u = mx_kscale(H)[:, None]
    d = {}
    d["tab_words"], d["tab_scales"] = pack_weight(n((K, T)) * s, "e4m3")
    d["offs"] = striped(np.random.permutation(T)[:S])
    d["offs2"] = striped8(np.stack([np.random.permutation(T2)[:S] for _ in range(8)]))
    d["offs3"] = striped8(np.stack([np.random.permutation(T2)[:P] for _ in range(8)]))
    d["w1"] = (1.4 * n((K, H)) / K**0.5 / s).astype(np.float32)
    d["b1"] = (0.7 * n(H)).astype(np.float32)
    d["gain"] = (np.exp(0.3 * n(H)) * u[:, 0]).astype(np.float32)
    d["w2_words"], d["w2_scales"] = pack_weight(0.7 * n((K, H)) / K**0.5 / s * u.T, "e2m1")
    d["wgs"] = np.repeat(np.random.uniform(0.5, 2.0, (8, S)), 16, axis=0).astype(np.float32)
    d["wgt"] = np.repeat(np.random.uniform(0.5, 2.0, (8, P)), 16, axis=0).astype(np.float32)
    d["light"] = (0.9 * n((H, P)) * u).astype(np.float32)
    d["w3"] = (n((H, N)) / H**0.5 / u).astype(np.float32)
    d["w4_words"], d["w4_scales"] = pack_weight(0.8 * n((H, N)) / H**0.5 / u, "e4m3")
    d["w5"] = (n((K, N)) / K**0.5 / s).astype(np.float32)
    return d

def reference(tab_words, tab_scales, offs, offs2, offs3, w1, b1, gain, w2_words, w2_scales,
              wgs, wgt, light, w3, w4_words, w4_scales, w5):
    v = unpack_weight(tab_words, tab_scales, "e4m3")[:, unstriped(offs)]
    w2 = unpack_weight(w2_words, w2_scales, "e2m1")
    w4 = unpack_weight(w4_words, w4_scales, "e4m3")
    a = (mxq(f64(w1), 0, "e4m3").T @ v) + f64(b1)[:, None]
    bent = 0.5 * a * (1.0 + np.tanh(0.7978845608028654 * (a + 0.044715 * a**3)))
    h = f64(gain)[:, None] * bent + (w2.T @ v)
    page = put_heads(h, f64(wgs), unstriped8(offs2), T2)
    x = heads(page, f64(wgt), unstriped8(offs3))
    zq = mxq(x + f64(light), 0, "e4m3")
    stress = np.abs(mxq(f64(w3), 0, "e4m3").T @ zq)
    return stress + (w4.T @ zq + mxq(f64(w5), 0, "e4m3").T @ v)

@@ -1,0 +1,290 @@
+from contextlib import ExitStack
+
+import concourse.mybir as mybir
+from concourse.masks import make_identity
+
+K, T, S, H, T2, J, N = 512, 4096, 1024, 1024, 2048, 1024, 384
+FLOPS = 2 * (2 * K * H * S + 2 * H * N * J + K * N * S)
+
+F32 = mybir.dt.float32
+BF16 = mybir.dt.bfloat16
+I32 = mybir.dt.int32
+U32 = mybir.dt.uint32
+U16 = mybir.dt.uint16
+U8 = mybir.dt.uint8
+FP8X4 = mybir.dt.float8_e4m3fn_x4
+FP4X4 = mybir.dt.float4_e2m1fn_x4
+ACT = mybir.ActivationFunctionType
+ALU = mybir.AluOpType
+
+P = 128
+PACK = 4
+K_PASS = P * PACK
+BANK = 512
+SLICES = H // P
+PAGES = 4
+CHUNKS = (((0, 1024),), ((0, 512), (512, 256), (768, 256)))
+OUT_CHUNKS = CHUNKS[1]
+
+
+def tile_list_bonsai_vigour_rounds_kernel(
+    tc, tab_words, tab_scales, offs, offs2, offs3, w1, b1, gain, w2_words, w2_scales,
+    wgs, wgt, light, w3, w4_words, w4_scales, w5, out,
+):
+    nc = tc.nc
+    with ExitStack() as ctx:
+        keep = ctx.enter_context(tc.tile_pool(name="keep", bufs=1))
+        ring = ctx.enter_context(tc.tile_pool(name="ring", bufs=2))
+        psum = ctx.enter_context(tc.psum_pool(name="psum", bufs=2))
+
+        def held(shape, dtype, name):
+            return keep.tile(shape, dtype, name=name, align_bytes=64)
+
+        idx = held([P, S // 16], U16, "idx")
+        idx_put = held([P, S // 16], U16, "idx_put")
+        idx_read = held([P, J // 16], U16, "idx_read")
+        table = held([P, T], I32, "table")
+        table_scales = held([P, T], U8, "table_scales")
+        w2_raw = held([P, 2 * H], U8, "w2_raw")
+        w2_raw_scales = held([P, H], U8, "w2_raw_scales")
+        w4_codes = held([P, 2, N], I32, "w4_codes")
+        w4_planes = held([P, N], U8, "w4_planes")
+        w1_raw = [held([P, PACK, K_PASS], F32, "w1_raw%d" % b) for b in range(2)]
+        late_raw = [held([P, PACK, N], F32, "late_raw%d" % a) for a in range(3)]
+        light_sb = [held([P, PACK, J], F32, "light%d" % b) for b in range(2)]
+        bias = held([P, 2, PACK], F32, "bias")
+        gains = held([P, 2, PACK], F32, "gains")
+        put_weight = held([P, S], F32, "put_weight")
+        read_weight = held([P, J], F32, "read_weight")
+        pages = [held([P, T2], F32, "page%d" % n) for n in range(PAGES)]
+        identity = held([P, P], F32, "identity")
+
+        nc.vector.memset(table_scales[:].bitcast(I32), 0)
+        nc.gpsimd.memset(w2_raw_scales[:].bitcast(I32), 0)
+
+        nc.sync.dma_start(idx[:], offs)
+        nc.sync.dma_start(table[:], tab_words[0].rearrange("p t i -> p (t i)").bitcast(I32))
+        for q in range(4):
+            nc.sync.dma_start(table_scales[32 * q : 32 * q + 4, :].bitcast(I32), tab_scales[0, 4 * q : 4 * q + 4, :].bitcast(I32))
+        nc.sync.dma_start(w1_raw[0][:], w1[:, 0:K_PASS].rearrange("(p i) c -> p i c", i=PACK))
+        nc.sync.dma_start(w2_raw[:].bitcast(I32), w2_words[0].bitcast(I32))
+        for q in range(4):
+            nc.gpsimd.dma_start(w2_raw_scales[32 * q : 32 * q + 4, :].bitcast(I32), w2_scales[0, 4 * q : 4 * q + 4, :].bitcast(I32))
+        nc.gpsimd.dma_start(bias[:], b1.rearrange("(b p i) -> p b i", b=2, i=PACK))
+        nc.gpsimd.dma_start(gains[:], gain.rearrange("(b p i) -> p b i", b=2, i=PACK))
+        nc.sync.dma_start(idx_put[:], offs2)
+        nc.sync.dma_start(put_weight[:], wgs)
+        nc.sync.dma_start(idx_read[:], offs3)
+        nc.sync.dma_start(read_weight[:], wgt)
+        nc.sync.dma_start(w1_raw[1][:], w1[:, K_PASS:H].rearrange("(p i) c -> p i c", i=PACK))
+        nc.sync.dma_start(light_sb[0][:], light[0:K_PASS, :].rearrange("(p i) j -> p i j", i=PACK))
+        late_rows = (w3[0:K_PASS, :], w3[K_PASS:H, :], w5)
+        for a in range(3):
+            nc.sync.dma_start(late_raw[a][:], late_rows[a].rearrange("(p i) n -> p i n", i=PACK))
+        nc.sync.dma_start(light_sb[1][:], light[K_PASS:H, :].rearrange("(p i) j -> p i j", i=PACK))
+        nc.sync.dma_start(w4_codes[:], w4_words.rearrange("a p c i -> p a (c i)").bitcast(I32))
+        nc.vector.memset(w4_planes[:].bitcast(I32), 0)
+        for q in range(4):
+            nc.sync.dma_start(w4_planes[32 * q : 32 * q + 8, :].bitcast(I32), w4_scales[:, 4 * q : 4 * q + 4, :].bitcast(I32))
+
+        for page in pages:
+            nc.vector.memset(page[:], 0.0)
+        make_identity(nc, identity[:])
+
+        w2_codes = held([P, 2 * H], U8, "w2_codes")
+        w2_plane = held([P, H], U8, "w2_plane")
+        nc.vector.tensor_copy(
+            w2_codes[:].rearrange("p (b i m e) -> p b i m e", b=2, i=PACK, e=2),
+            w2_raw[:].rearrange("p (b m i e) -> p b i m e", b=2, i=PACK, e=2),
+        )
+        nc.vector.tensor_copy(
+            w2_plane[:].rearrange("p (b i m) -> p b i m", b=2, i=PACK),
+            w2_raw_scales[:].rearrange("p (b m i) -> p b i m", b=2, i=PACK),
+        )
+
+        v_codes = [held([P, BANK], I32, "v_codes%d" % c) for c in range(2)]
+        v_plane = [held([P, BANK], U8, "v_plane%d" % c) for c in range(2)]
+
+        def pick_table(c):
+            entries = idx[:, c * BANK // 16 : (c + 1) * BANK // 16]
+            nc.vector.tensor_copy(v_codes[c][:].bitcast(U32), table[:].bitcast(U32).indirect(entries))
+            nc.vector.tensor_copy(v_plane[c][:], table_scales[:].indirect(entries))
+
+        w1_codes = [held([P, 2 * P], U32, "w1_codes%d" % n) for n in range(4)]
+        w1_plane = [held([P, 2 * P], U8, "w1_plane%d" % n) for n in range(4)]
+        w1_round = [held([P, 2 * P * PACK], BF16, "w1_round%d" % n) for n in range(4)]
+
+        def round_w1(n):
+            b, pair = divmod(n, 2)
+            nc.scalar.copy(
+                w1_round[n][:].rearrange("p (e m i) -> p m i e", e=2, i=PACK),
+                w1_raw[b][:].rearrange("p i (m t) -> p m i t", t=PACK)[:, :, :, 2 * pair : 2 * pair + 2],
+            )
+
+        def quantize_w1(n):
+            nc.vector.quantize_mx(out=w1_codes[n][:].bitcast(FP8X4), scales=w1_plane[n][:], in_=w1_round[n][:])
+
+        late_round = held([P, 3 * N * PACK], BF16, "late_round")
+        late_codes = held([P, 3 * N], U32, "late_codes")
+        late_plane = held([P, 3 * N], U8, "late_plane")
+
+        def round_late(a):
+            nc.scalar.copy(
+                late_round[:, a * N * PACK : (a + 1) * N * PACK].rearrange("p (c e i) -> p c i e", e=4, i=PACK),
+                late_raw[a][:].rearrange("p i (c e) -> p c i e", e=4),
+            )
+
+        def quantize_late(first, count):
+            nc.vector.quantize_mx(
+                out=late_codes[:, first : first + count].bitcast(FP8X4),
+                scales=late_plane[:, first : first + count],
+                in_=late_round[:, PACK * first : PACK * (first + count)],
+            )
+
+        features = {}
+
+        def make_features(s):
+            b, i = divmod(s, PACK)
+            h = ring.tile([P, S], F32, name="h")
+            features[s] = h
+            w1_cols = slice((s % 2) * P, (s % 2 + 1) * P)
+            for c in range(2):
+                cols = slice(c * BANK, (c + 1) * BANK)
+                pre = psum.tile([P, BANK], F32, name="sum_a")
+                skip = psum.tile([P, BANK], F32, name="sum_b")
+                nc.tensor.matmul_mx(
+                    out=pre[:], lhsT=w1_codes[s // 2][:, w1_cols].bitcast(FP8X4), lhsT_scale=w1_plane[s // 2][:, w1_cols],
+                    rhs=v_codes[c][:].bitcast(FP8X4), rhs_scale=v_plane[c][:], start=True, stop=True,
+                )
+                nc.tensor.matmul_mx(
+                    out=skip[:], lhsT=w2_codes[:, 2 * P * s : 2 * P * (s + 1)].bitcast(FP4X4),
+                    lhsT_scale=w2_plane[:, P * s : P * (s + 1)],
+                    rhs=v_codes[c][:].bitcast(FP8X4), rhs_scale=v_plane[c][:], start=True, stop=True,
+                )
+                bent = ring.tile([P, BANK], F32, name="bent")
+                nc.scalar.activation(bent[:], pre[:], ACT.Gelu_apprx_tanh, bias=bias[:, b, i : i + 1])
+                nc.vector.scalar_tensor_tensor(h[:, cols], bent[:], gains[:, b, i : i + 1], skip[:], ALU.mult, ALU.add)
+
+        def put(s):
+            nc.vector.tensor_tensor(pages[s % PAGES][:].indirect(idx_put[:]), features[s][:], put_weight[:], ALU.mult)
+
+        x = [held([P, PACK, J], F32, "x")] * 2
+
+        def read(s, first, width):
+            b, i = divmod(s, PACK)
+            cols = slice(first, first + width)
+            nc.vector.tensor_tensor(
+                x[b][:, i, cols],
+                pages[s % PAGES][:].indirect(idx_read[:, first // 16 : (first + width) // 16]),
+                read_weight[:, cols],
+                ALU.mult,
+            )
+
+        z_round = [held([P, J * PACK], BF16, "z_round")] * 2
+        z_codes = [held([P, J], U32, "z_codes%d" % b) for b in range(2)]
+        z_plane = [held([P, J], U8, "z_plane%d" % b) for b in range(2)]
+
+        def add_light(b, first):
+            back = psum.tile([P, 2, 2, P], F32, name="back")
+            for c in range(2):
+                cols = slice(first + c * P, first + (c + 1) * P)
+                turned = psum.tile([P, PACK, P], F32, name="turned")
+                terms = [(light_sb[b], i) for i in range(PACK)] + [(x[b], i) for i in range(PACK)]
+                for n, (term, i) in enumerate(terms):
+                    nc.tensor.matmul(
+                        turned[:, i, :], term[:, i, cols], identity[:], is_transpose=True,
+                        start=(n == 0), stop=(n == len(terms) - 1),
+                    )
+                pairs = ring.tile([P, 2, P, 2], BF16, name="pairs")
+                nc.scalar.copy(pairs[:], turned[:].rearrange("j (u e) p -> j u p e", e=2))
+                for u in range(2):
+                    nc.tensor.transpose(back[:, c, u, :], pairs[:, u].rearrange("j p e -> j (p e)").bitcast(F32), identity[:])
+            words = z_round[b][:, PACK * first : PACK * (first + 2 * P)].bitcast(F32)
+            nc.scalar.copy(words.rearrange("p (c j u) -> p c j u", c=2, u=2), back[:].rearrange("p c u j -> p c j u"))
+
+        def quantize_z(b, first, width):
+            nc.vector.quantize_mx(
+                out=z_codes[b][:, first : first + width].bitcast(FP8X4),
+                scales=z_plane[b][:, first : first + width],
+                in_=z_round[b][:, PACK * first : PACK * (first + width)],
+            )
+
+        def score(first, width):
+            cols = slice(first, first + width)
+            half, within = divmod(first, BANK)
+            v_cols = slice(within, within + width)
+            for n0 in range(0, N, P):
+                stress = psum.tile([P, BANK], F32, name="sum_a")
+                rest = psum.tile([P, BANK], F32, name="sum_b")
+                w5_cols = slice(2 * N + n0, 2 * N + n0 + P)
+                nc.tensor.matmul_mx(
+                    out=rest[:, 0:width], lhsT=late_codes[:, w5_cols].bitcast(FP8X4), lhsT_scale=late_plane[:, w5_cols],
+                    rhs=v_codes[half][:, v_cols].bitcast(FP8X4), rhs_scale=v_plane[half][:, v_cols], start=True, stop=False,
+                )
+                for b in range(2):
+                    w3_cols = slice(b * N + n0, b * N + n0 + P)
+                    nc.tensor.matmul_mx(
+                        out=stress[:, 0:width], lhsT=late_codes[:, w3_cols].bitcast(FP8X4), lhsT_scale=late_plane[:, w3_cols],
+                        rhs=z_codes[b][:, cols].bitcast(FP8X4), rhs_scale=z_plane[b][:, cols], start=(b == 0), stop=(b == 1),
+                    )
+                    nc.tensor.matmul_mx(
+                        out=rest[:, 0:width], lhsT=w4_codes[:, b, n0 : n0 + P].bitcast(FP8X4),
+                        lhsT_scale=w4_planes[4 * b : P, n0 : n0 + P],
+                        rhs=z_codes[b][:, cols].bitcast(FP8X4), rhs_scale=z_plane[b][:, cols], start=False, stop=(b == 1),
+                    )
+                size = ring.tile([P, BANK], F32, name="size")
+                nc.scalar.activation(size[:, 0:width], stress[:, 0:width], ACT.Abs)
+                result = ring.tile([P, BANK], F32, name="result", bufs=3)
+                nc.vector.tensor_tensor(result[:, 0:width], size[:, 0:width], rest[:, 0:width], ALU.add)
+                nc.sync.dma_start(out[n0 : n0 + P, cols], result[:, 0:width])
+
+        pick_table(0)
+        round_w1(0)
+        round_w1(1)
+        quantize_w1(0)
+        pick_table(1)
+        make_features(0)
+        put(0)
+        make_features(1)
+        quantize_w1(1)
+        round_w1(2)
+        round_w1(3)
+        put(1)
+        make_features(2)
+        read(0, 0, J)
+        quantize_w1(2)
+        put(2)
+        make_features(3)
+        read(1, 0, J)
+        quantize_w1(3)
+        for a in range(3):
+            round_late(a)
+        put(3)
+        make_features(4)
+        read(2, 0, J)
+        put(4)
+        make_features(5)
+        read(3, 0, J)
+        put(5)
+        make_features(6)
+        quantize_late(0, 512)
+        quantize_late(512, 512)
+        quantize_late(1024, 128)
+        for first in range(0, J, 2 * P):
+            add_light(0, first)
+        put(6)
+        make_features(7)
+        quantize_z(0, 0, 512)
+        quantize_z(0, 512, 512)
+        put(7)
+        done = None
+        for first, width in OUT_CHUNKS:
+            for s in range(PACK, SLICES):
+                read(s, first, width)
+            if done is not None:
+                score(*done)
+            for j0 in range(first, first + width, 2 * P):
+                add_light(1, j0)
+            quantize_z(1, first, width)
+            done = (first, width)
+        score(*done)

@@ -23,8 +23,8 @@ K_PASS = P * PACK
 BANK = 512
 SLICES = H // P
 PAGES = 4
-CHUNKS = (((0, 1024),), ((0, 512), (512, 256), (768, 256)))
-OUT_CHUNKS = CHUNKS[1]
+DIRECT_SLICES = (0, 1, 6, 7)
+CHUNK = 256
 
 
 def tile_list_bonsai_vigour_rounds_kernel(
@@ -49,34 +49,41 @@ def tile_list_bonsai_vigour_rounds_kernel(
         w2_raw_scales = held([P, H], U8, "w2_raw_scales")
         w4_codes = held([P, 2, N], I32, "w4_codes")
         w4_planes = held([P, N], U8, "w4_planes")
-        w1_raw = [held([P, PACK, K_PASS], F32, "w1_raw%d" % b) for b in range(2)]
+        w1_raw = {}
+
+        def load_w1(b):
+            w1_raw[b] = held([P, PACK, K_PASS], F32, ("w1_raw", "z_round")[b])
+            nc.sync.dma_start(w1_raw[b][:], w1[:, b * K_PASS : (b + 1) * K_PASS].rearrange("(p i) c -> p i c", i=PACK))
+
         late_raw = [held([P, PACK, N], F32, "late_raw%d" % a) for a in range(3)]
         light_sb = [held([P, PACK, J], F32, "light%d" % b) for b in range(2)]
         bias = held([P, 2, PACK], F32, "bias")
         gains = held([P, 2, PACK], F32, "gains")
         put_weight = held([P, S], F32, "put_weight")
         read_weight = held([P, J], F32, "read_weight")
-        pages = [held([P, T2], F32, "page%d" % n) for n in range(PAGES)]
+        pages = {n: held([P, T2], F32, "page%d" % n) for n in range(2)}
         identity = held([P, P], F32, "identity")
 
-        nc.vector.memset(table_scales[:].bitcast(I32), 0)
-        nc.gpsimd.memset(w2_raw_scales[:].bitcast(I32), 0)
+        def load_scale_rows(plane, rows):
+            for q in range(4):
+                nc.sync.dma_start(
+                    plane[32 * q : 32 * (q + 1), :].bitcast(I32),
+                    rows[4 * q : 4 * q + 4, :].bitcast(I32).partition_broadcast(8),
+                )
 
         nc.sync.dma_start(idx[:], offs)
-        nc.sync.dma_start(table[:], tab_words[0].rearrange("p t i -> p (t i)").bitcast(I32))
-        for q in range(4):
-            nc.sync.dma_start(table_scales[32 * q : 32 * q + 4, :].bitcast(I32), tab_scales[0, 4 * q : 4 * q + 4, :].bitcast(I32))
-        nc.sync.dma_start(w1_raw[0][:], w1[:, 0:K_PASS].rearrange("(p i) c -> p i c", i=PACK))
+        load_scale_rows(w2_raw_scales, w2_scales[0])
         nc.sync.dma_start(w2_raw[:].bitcast(I32), w2_words[0].bitcast(I32))
-        for q in range(4):
-            nc.gpsimd.dma_start(w2_raw_scales[32 * q : 32 * q + 4, :].bitcast(I32), w2_scales[0, 4 * q : 4 * q + 4, :].bitcast(I32))
-        nc.gpsimd.dma_start(bias[:], b1.rearrange("(b p i) -> p b i", b=2, i=PACK))
-        nc.gpsimd.dma_start(gains[:], gain.rearrange("(b p i) -> p b i", b=2, i=PACK))
+        nc.sync.dma_start(table[:], tab_words[0].rearrange("p t i -> p (t i)").bitcast(I32))
+        load_scale_rows(table_scales, tab_scales[0])
+        load_w1(0)
+        nc.sync.dma_start(bias[:], b1.rearrange("(b p i) -> p b i", b=2, i=PACK))
+        nc.sync.dma_start(gains[:], gain.rearrange("(b p i) -> p b i", b=2, i=PACK))
         nc.sync.dma_start(idx_put[:], offs2)
         nc.sync.dma_start(put_weight[:], wgs)
         nc.sync.dma_start(idx_read[:], offs3)
         nc.sync.dma_start(read_weight[:], wgt)
-        nc.sync.dma_start(w1_raw[1][:], w1[:, K_PASS:H].rearrange("(p i) c -> p i c", i=PACK))
+        load_w1(1)
         nc.sync.dma_start(light_sb[0][:], light[0:K_PASS, :].rearrange("(p i) j -> p i j", i=PACK))
         late_rows = (w3[0:K_PASS, :], w3[K_PASS:H, :], w5)
         for a in range(3):
@@ -87,15 +94,15 @@ def tile_list_bonsai_vigour_rounds_kernel(
         for q in range(4):
             nc.sync.dma_start(w4_planes[32 * q : 32 * q + 8, :].bitcast(I32), w4_scales[:, 4 * q : 4 * q + 4, :].bitcast(I32))
 
-        for page in pages:
-            nc.vector.memset(page[:], 0.0)
+        for n in range(2):
+            nc.vector.memset(pages[n][:], 0.0)
         make_identity(nc, identity[:])
 
         w2_codes = held([P, 2 * H], U8, "w2_codes")
         w2_plane = held([P, H], U8, "w2_plane")
         nc.vector.tensor_copy(
-            w2_codes[:].rearrange("p (b i m e) -> p b i m e", b=2, i=PACK, e=2),
-            w2_raw[:].rearrange("p (b m i e) -> p b i m e", b=2, i=PACK, e=2),
+            w2_codes[:].bitcast(U16).rearrange("p (b i m) -> p b i m", b=2, i=PACK),
+            w2_raw[:].bitcast(U16).rearrange("p (b m i) -> p b i m", b=2, i=PACK),
         )
         nc.vector.tensor_copy(
             w2_plane[:].rearrange("p (b i m) -> p b i m", b=2, i=PACK),
@@ -112,7 +119,7 @@ def tile_list_bonsai_vigour_rounds_kernel(
 
         w1_codes = [held([P, 2 * P], U32, "w1_codes%d" % n) for n in range(4)]
         w1_plane = [held([P, 2 * P], U8, "w1_plane%d" % n) for n in range(4)]
-        w1_round = [held([P, 2 * P * PACK], BF16, "w1_round%d" % n) for n in range(4)]
+        w1_round = [held([P, 2 * P * PACK], BF16, ("w1_round0", "w1_round1", "w1_round2", "page2")[n]) for n in range(4)]
 
         def round_w1(n):
             b, pair = divmod(n, 2)
@@ -141,11 +148,28 @@ def tile_list_bonsai_vigour_rounds_kernel(
                 in_=late_round[:, PACK * first : PACK * (first + count)],
             )
 
+        def clear_page(n):
+            pages[n] = held([P, T2], F32, "page%d" % n)
+            nc.gpsimd.memset(pages[n][:], 0.0)
+
         features = {}
+
+        def put_entries(s, first, count):
+            nc.vector.tensor_tensor(
+                pages[s % PAGES][:].indirect(idx_put[:, first // 16 : (first + count) // 16]),
+                features[s][:, first : first + count],
+                put_weight[:, first : first + count],
+                ALU.mult,
+            )
 
         def make_features(s):
             b, i = divmod(s, PACK)
-            h = ring.tile([P, S], F32, name="h")
+            if s == 1:
+                h = held([P, S], F32, "page3")
+            elif s == SLICES - 1:
+                h = held([P, S], F32, "x")
+            else:
+                h = ring.tile([P, S], F32, name="h", bufs=3)
             features[s] = h
             w1_cols = slice((s % 2) * P, (s % 2 + 1) * P)
             for c in range(2):
@@ -156,57 +180,107 @@ def tile_list_bonsai_vigour_rounds_kernel(
                     out=pre[:], lhsT=w1_codes[s // 2][:, w1_cols].bitcast(FP8X4), lhsT_scale=w1_plane[s // 2][:, w1_cols],
                     rhs=v_codes[c][:].bitcast(FP8X4), rhs_scale=v_plane[c][:], start=True, stop=True,
                 )
-                nc.tensor.matmul_mx(
-                    out=skip[:], lhsT=w2_codes[:, 2 * P * s : 2 * P * (s + 1)].bitcast(FP4X4),
-                    lhsT_scale=w2_plane[:, P * s : P * (s + 1)],
-                    rhs=v_codes[c][:].bitcast(FP8X4), rhs_scale=v_plane[c][:], start=True, stop=True,
-                )
+                w2_slice = w2_codes[:, 2 * P * s : 2 * P * (s + 1)].bitcast(FP4X4)
+                w2_slice_plane = w2_plane[:, P * s : P * (s + 1)]
                 bent = ring.tile([P, BANK], F32, name="bent")
                 nc.scalar.activation(bent[:], pre[:], ACT.Gelu_apprx_tanh, bias=bias[:, b, i : i + 1])
-                nc.vector.scalar_tensor_tensor(h[:, cols], bent[:], gains[:, b, i : i + 1], skip[:], ALU.mult, ALU.add)
+                if s in DIRECT_SLICES:
+                    nc.tensor.matmul_mx(
+                        out=skip[:], lhsT=w2_slice, lhsT_scale=w2_slice_plane,
+                        rhs=v_codes[c][:].bitcast(FP8X4), rhs_scale=v_plane[c][:], start=True, stop=True,
+                    )
+                    nc.vector.scalar_tensor_tensor(h[:, cols], bent[:], gains[:, b, i : i + 1], skip[:], ALU.mult, ALU.add)
+                    if s == 0:
+                        put_entries(s, c * BANK, BANK)
+                    continue
+                blocks = [slice(n * P, (n + 1) * P) for n in range(BANK // P)]
+                for block in blocks:
+                    nc.tensor.matmul_mx(
+                        out=skip[:, block], lhsT=v_codes[c][:, block].bitcast(FP8X4), lhsT_scale=v_plane[c][:, block],
+                        rhs=w2_slice, rhs_scale=w2_slice_plane, start=True, stop=True,
+                    )
+                skip_t = ring.tile([P, BANK], F32, name="skip_t")
+                nc.scalar.copy(skip_t[:], skip[:])
+                scaled = ring.tile([P, BANK], F32, name="scaled")
+                nc.scalar.activation(scaled[:], bent[:], ACT.Copy, scale=gains[:, b, i : i + 1])
+                turned = psum.tile([P, BANK], F32, name="turned")
+                for block in blocks:
+                    nc.tensor.transpose(turned[:, block], scaled[:, block], identity[:])
+                scaled_t = ring.tile([P, BANK], F32, name="scaled_t")
+                nc.scalar.copy(scaled_t[:], turned[:])
+                back = psum.tile([P, BANK], F32, name="back")
+                terms = [(term, block) for term in (skip_t, scaled_t) for block in blocks]
+                for n, (term, block) in enumerate(terms):
+                    nc.tensor.matmul(
+                        back[:, block], term[:, block], identity[:], is_transpose=True,
+                        start=(n == 0), stop=(n == len(terms) - 1),
+                    )
+                nc.scalar.copy(h[:, cols], back[:])
 
         def put(s):
-            nc.vector.tensor_tensor(pages[s % PAGES][:].indirect(idx_put[:]), features[s][:], put_weight[:], ALU.mult)
+            put_entries(s, 0, S)
 
-        x = [held([P, PACK, J], F32, "x")] * 2
-
-        def read(s, first, width):
-            b, i = divmod(s, PACK)
-            cols = slice(first, first + width)
+        def read(s, x_plane, first):
+            width = x_plane.shape[1]
             nc.vector.tensor_tensor(
-                x[b][:, i, cols],
+                x_plane,
                 pages[s % PAGES][:].indirect(idx_read[:, first // 16 : (first + width) // 16]),
-                read_weight[:, cols],
+                read_weight[:, first : first + width],
                 ALU.mult,
             )
 
-        z_round = [held([P, J * PACK], BF16, "z_round")] * 2
         z_codes = [held([P, J], U32, "z_codes%d" % b) for b in range(2)]
         z_plane = [held([P, J], U8, "z_plane%d" % b) for b in range(2)]
 
-        def add_light(b, first):
+        def add_light(b, x, z_round, first):
             back = psum.tile([P, 2, 2, P], F32, name="back")
             for c in range(2):
-                cols = slice(first + c * P, first + (c + 1) * P)
                 turned = psum.tile([P, PACK, P], F32, name="turned")
-                terms = [(light_sb[b], i) for i in range(PACK)] + [(x[b], i) for i in range(PACK)]
+                terms = [(light_sb[b][:, i, first + c * P : first + (c + 1) * P], i) for i in range(PACK)]
+                terms.extend((x[:, i, c * P : (c + 1) * P], i) for i in range(PACK))
                 for n, (term, i) in enumerate(terms):
                     nc.tensor.matmul(
-                        turned[:, i, :], term[:, i, cols], identity[:], is_transpose=True,
+                        turned[:, i, :], term, identity[:], is_transpose=True,
                         start=(n == 0), stop=(n == len(terms) - 1),
                     )
                 pairs = ring.tile([P, 2, P, 2], BF16, name="pairs")
                 nc.scalar.copy(pairs[:], turned[:].rearrange("j (u e) p -> j u p e", e=2))
                 for u in range(2):
                     nc.tensor.transpose(back[:, c, u, :], pairs[:, u].rearrange("j p e -> j (p e)").bitcast(F32), identity[:])
-            words = z_round[b][:, PACK * first : PACK * (first + 2 * P)].bitcast(F32)
-            nc.scalar.copy(words.rearrange("p (c j u) -> p c j u", c=2, u=2), back[:].rearrange("p c u j -> p c j u"))
+            nc.scalar.copy(
+                z_round.bitcast(F32).rearrange("p (c j u) -> p c j u", c=2, u=2), back[:].rearrange("p c u j -> p c j u")
+            )
 
-        def quantize_z(b, first, width):
+        def add_light_first_pair(x_pair, words, first):
+            back = psum.tile([P, BANK], F32, name="back")
+            for half in range(2):
+                turned = psum.tile([P, 2, 2, P], F32, name="turned")
+                start = first + half * 2 * P
+                terms = [
+                    (term[:, e, start + c * P : start + (c + 1) * P], c, e)
+                    for term in (light_sb[1], x_pair) for c in range(2) for e in range(2)
+                ]
+                for n, (term, c, e) in enumerate(terms):
+                    nc.tensor.matmul(
+                        turned[:, c, e, :], term, identity[:], is_transpose=True,
+                        start=(n == 0), stop=(n == len(terms) - 1),
+                    )
+                pairs = ring.tile([P, 2, P, 2], BF16, name="pairs")
+                nc.scalar.copy(pairs[:], turned[:].rearrange("j c e p -> j c p e"))
+                for c in range(2):
+                    column = (2 * half + c) * P
+                    nc.tensor.transpose(
+                        back[:, column : column + P], pairs[:, c].rearrange("j p e -> j (p e)").bitcast(F32), identity[:]
+                    )
+            for half in range(2):
+                nc.scalar.copy(words[first // CHUNK + half][:, 0, :], back[:, half * CHUNK : (half + 1) * CHUNK])
+
+        def quantize_z(b, z_round, first):
+            width = z_round.shape[1] // PACK
             nc.vector.quantize_mx(
                 out=z_codes[b][:, first : first + width].bitcast(FP8X4),
                 scales=z_plane[b][:, first : first + width],
-                in_=z_round[b][:, PACK * first : PACK * (first + width)],
+                in_=z_round,
             )
 
         def score(first, width):
@@ -214,77 +288,90 @@ def tile_list_bonsai_vigour_rounds_kernel(
             half, within = divmod(first, BANK)
             v_cols = slice(within, within + width)
             for n0 in range(0, N, P):
-                stress = psum.tile([P, BANK], F32, name="sum_a")
-                rest = psum.tile([P, BANK], F32, name="sum_b")
+                sums = psum.tile([P, BANK], F32, name=("sum_a", "sum_b", "turned", "back")[(3 * first // width + n0 // P) % 4])
+                stress, rest = sums[:, 0:width], sums[:, width : 2 * width]
                 w5_cols = slice(2 * N + n0, 2 * N + n0 + P)
                 nc.tensor.matmul_mx(
-                    out=rest[:, 0:width], lhsT=late_codes[:, w5_cols].bitcast(FP8X4), lhsT_scale=late_plane[:, w5_cols],
+                    out=rest, lhsT=late_codes[:, w5_cols].bitcast(FP8X4), lhsT_scale=late_plane[:, w5_cols],
                     rhs=v_codes[half][:, v_cols].bitcast(FP8X4), rhs_scale=v_plane[half][:, v_cols], start=True, stop=False,
                 )
                 for b in range(2):
                     w3_cols = slice(b * N + n0, b * N + n0 + P)
                     nc.tensor.matmul_mx(
-                        out=stress[:, 0:width], lhsT=late_codes[:, w3_cols].bitcast(FP8X4), lhsT_scale=late_plane[:, w3_cols],
-                        rhs=z_codes[b][:, cols].bitcast(FP8X4), rhs_scale=z_plane[b][:, cols], start=(b == 0), stop=(b == 1),
+                        out=stress, lhsT=late_codes[:, w3_cols].bitcast(FP8X4), lhsT_scale=late_plane[:, w3_cols],
+                        rhs=z_codes[b][:, cols].bitcast(FP8X4), rhs_scale=z_plane[b][:, cols], start=False, stop=False,
                     )
                     nc.tensor.matmul_mx(
-                        out=rest[:, 0:width], lhsT=w4_codes[:, b, n0 : n0 + P].bitcast(FP8X4),
+                        out=rest, lhsT=w4_codes[:, b, n0 : n0 + P].bitcast(FP8X4),
                         lhsT_scale=w4_planes[4 * b : P, n0 : n0 + P],
                         rhs=z_codes[b][:, cols].bitcast(FP8X4), rhs_scale=z_plane[b][:, cols], start=False, stop=(b == 1),
                     )
-                size = ring.tile([P, BANK], F32, name="size")
-                nc.scalar.activation(size[:, 0:width], stress[:, 0:width], ACT.Abs)
-                result = ring.tile([P, BANK], F32, name="result", bufs=3)
-                nc.vector.tensor_tensor(result[:, 0:width], size[:, 0:width], rest[:, 0:width], ALU.add)
+                size = ring.tile([P, width], F32, name="size")
+                nc.scalar.activation(size[:, 0:width], stress, ACT.Abs)
+                result = ring.tile([P, width], F32, name="result", bufs=3)
+                nc.vector.tensor_tensor(result[:, 0:width], size[:, 0:width], rest, ALU.add)
                 nc.sync.dma_start(out[n0 : n0 + P, cols], result[:, 0:width])
 
+        x = held([P, PACK, J], F32, "x")
         pick_table(0)
         round_w1(0)
-        round_w1(1)
         quantize_w1(0)
         pick_table(1)
         make_features(0)
-        put(0)
-        make_features(1)
+        round_w1(1)
         quantize_w1(1)
+        make_features(1)
         round_w1(2)
         round_w1(3)
-        put(1)
-        make_features(2)
-        read(0, 0, J)
         quantize_w1(2)
-        put(2)
-        make_features(3)
-        read(1, 0, J)
         quantize_w1(3)
+        clear_page(2)
+        make_features(2)
+        put(1)
+        clear_page(3)
+        make_features(3)
+        read(0, x[:, 0, :], 0)
+        put(2)
+        make_features(4)
         for a in range(3):
             round_late(a)
+        read(1, x[:, 1, :], 0)
         put(3)
-        make_features(4)
-        read(2, 0, J)
-        put(4)
         make_features(5)
-        read(3, 0, J)
-        put(5)
+        read(2, x[:, 2, :], 0)
+        read(3, x[:, 3, :], 0)
+        put(4)
         make_features(6)
         quantize_late(0, 512)
         quantize_late(512, 512)
         quantize_late(1024, 128)
+        put(5)
+        z_round = held([P, J * PACK], BF16, "z_round")
+        x_pair = held([P, 2, J], F32, "table")
+        read(4, x_pair[:, 0, :], 0)
+        read(5, x_pair[:, 1, :], 0)
         for first in range(0, J, 2 * P):
-            add_light(0, first)
-        put(6)
+            add_light(0, x[:, :, first : first + 2 * P], z_round[:, PACK * first : PACK * (first + 2 * P)], first)
         make_features(7)
-        quantize_z(0, 0, 512)
-        quantize_z(0, 512, 512)
+        put(6)
+        z_words = [held([P, 2, CHUNK], F32, ("w1_round0", "w1_round1", "w1_round2", "w2_raw")[c]) for c in range(J // CHUNK)]
+        for first in range(0, J, BANK):
+            add_light_first_pair(x_pair, z_words, first)
+        quantize_z(0, z_round[:, 0:2048], 0)
+        quantize_z(0, z_round[:, 2048:4096], 512)
         put(7)
-        done = None
-        for first, width in OUT_CHUNKS:
-            for s in range(PACK, SLICES):
-                read(s, first, width)
-            if done is not None:
-                score(*done)
-            for j0 in range(first, first + width, 2 * P):
-                add_light(1, j0)
-            quantize_z(1, first, width)
-            done = (first, width)
-        score(*done)
+        x_last = held([P, J // CHUNK, 2, CHUNK], F32, "x")
+        for c in range(J // CHUNK):
+            cols = slice(c * CHUNK, (c + 1) * CHUNK)
+            for e in range(2):
+                read(6 + e, x_last[:, c, e, :], c * CHUNK)
+            nc.vector.tensor_tensor(
+                z_words[c][:, 1, :].bitcast(BF16).rearrange("p (j e) -> p j e", e=2),
+                x_last[:, c].rearrange("p e j -> p j e"),
+                light_sb[1][:, 2:4, cols].rearrange("p e j -> p j e"),
+                ALU.add,
+            )
+            z_chunk = ring.tile([P, CHUNK * PACK], BF16, name="z_chunk", align_bytes=64)
+            nc.scalar.copy(z_chunk[:].bitcast(F32).rearrange("p (j u) -> p j u", u=2), z_words[c][:].rearrange("p u j -> p j u"))
+            quantize_z(1, z_chunk[:], c * CHUNK)
+            score(c * CHUNK, CHUNK)

@@ -23,7 +23,7 @@ K_PASS = P * PACK
 BANK = 512
 SLICES = H // P
 PAGES = 4
-DIRECT_SLICES = (0, 1, 6, 7)
+DIRECT_SLICES = (0, 1, 7)
 CHUNK = 256
 
 
@@ -57,28 +57,31 @@ def tile_list_bonsai_vigour_rounds_kernel(
 
         late_raw = [held([P, PACK, N], F32, "late_raw%d" % a) for a in range(3)]
         light_sb = [held([P, PACK, J], F32, "light%d" % b) for b in range(2)]
-        bias = held([P, 2, PACK], F32, "bias")
-        gains = held([P, 2, PACK], F32, "gains")
+        bias = held([P, 2, 2 * PACK], F32, "bias")
+        gains = held([P, 2, 2 * PACK], F32, "gains")
         put_weight = held([P, S], F32, "put_weight")
         read_weight = held([P, J], F32, "read_weight")
         pages = {n: held([P, T2], F32, "page%d" % n) for n in range(2)}
         identity = held([P, P], F32, "identity")
 
-        def load_scale_rows(plane, rows):
+        def load_scale_rows(rows, name):
+            staged = held([P, rows.shape[1] // 4], I32, name)
             for q in range(4):
-                nc.sync.dma_start(
-                    plane[32 * q : 32 * (q + 1), :].bitcast(I32),
-                    rows[4 * q : 4 * q + 4, :].bitcast(I32).partition_broadcast(8),
-                )
+                nc.sync.dma_start(staged[32 * q : 32 * q + 4, :], rows[4 * q : 4 * q + 4, :].bitcast(I32))
+            return staged
 
-        nc.sync.dma_start(idx[:], offs)
-        load_scale_rows(w2_raw_scales, w2_scales[0])
+        def place_scale_rows(plane, staged):
+            for q in range(4):
+                nc.vector.tensor_copy(plane[32 * q : 32 * q + 4, :].bitcast(I32), staged[32 * q : 32 * q + 4, :])
+
+        w2_rows = load_scale_rows(w2_scales[0], "w2_rows")
+        table_rows = load_scale_rows(tab_scales[0], "table_rows")
         nc.sync.dma_start(w2_raw[:].bitcast(I32), w2_words[0].bitcast(I32))
         nc.sync.dma_start(table[:], tab_words[0].rearrange("p t i -> p (t i)").bitcast(I32))
-        load_scale_rows(table_scales, tab_scales[0])
+        nc.sync.dma_start(idx[:], offs)
         load_w1(0)
-        nc.sync.dma_start(bias[:], b1.rearrange("(b p i) -> p b i", b=2, i=PACK))
-        nc.sync.dma_start(gains[:], gain.rearrange("(b p i) -> p b i", b=2, i=PACK))
+        nc.sync.dma_start(bias[:, :, 0:PACK], b1.rearrange("(b p i) -> p b i", b=2, i=PACK))
+        nc.sync.dma_start(gains[:, :, 0:PACK], gain.rearrange("(b p i) -> p b i", b=2, i=PACK))
         nc.sync.dma_start(idx_put[:], offs2)
         nc.sync.dma_start(put_weight[:], wgs)
         nc.sync.dma_start(idx_read[:], offs3)
@@ -94,20 +97,27 @@ def tile_list_bonsai_vigour_rounds_kernel(
         for q in range(4):
             nc.sync.dma_start(w4_planes[32 * q : 32 * q + 8, :].bitcast(I32), w4_scales[:, 4 * q : 4 * q + 4, :].bitcast(I32))
 
+        nc.vector.memset(table_scales[:].bitcast(I32), 0)
+        nc.vector.memset(w2_raw_scales[:].bitcast(I32), 0)
         for n in range(2):
             nc.vector.memset(pages[n][:], 0.0)
+        place_scale_rows(w2_raw_scales, w2_rows)
+        place_scale_rows(table_scales, table_rows)
         make_identity(nc, identity[:])
 
         w2_codes = held([P, 2 * H], U8, "w2_codes")
         w2_plane = held([P, H], U8, "w2_plane")
-        nc.vector.tensor_copy(
-            w2_codes[:].bitcast(U16).rearrange("p (b i m) -> p b i m", b=2, i=PACK),
-            w2_raw[:].bitcast(U16).rearrange("p (b m i) -> p b i m", b=2, i=PACK),
-        )
-        nc.vector.tensor_copy(
-            w2_plane[:].rearrange("p (b i m) -> p b i m", b=2, i=PACK),
-            w2_raw_scales[:].rearrange("p (b m i) -> p b i m", b=2, i=PACK),
-        )
+
+        def deal_w2(b):
+            cols = slice(b * K_PASS, (b + 1) * K_PASS)
+            nc.vector.tensor_copy(
+                w2_codes[:].bitcast(U16)[:, cols].rearrange("p (i m) -> p i m", i=PACK),
+                w2_raw[:].bitcast(U16)[:, cols].rearrange("p (m i) -> p i m", i=PACK),
+            )
+            nc.vector.tensor_copy(
+                w2_plane[:, cols].rearrange("p (i m) -> p i m", i=PACK),
+                w2_raw_scales[:, cols].rearrange("p (m i) -> p i m", i=PACK),
+            )
 
         v_codes = [held([P, BANK], I32, "v_codes%d" % c) for c in range(2)]
         v_plane = [held([P, BANK], U8, "v_plane%d" % c) for c in range(2)]
@@ -119,7 +129,7 @@ def tile_list_bonsai_vigour_rounds_kernel(
 
         w1_codes = [held([P, 2 * P], U32, "w1_codes%d" % n) for n in range(4)]
         w1_plane = [held([P, 2 * P], U8, "w1_plane%d" % n) for n in range(4)]
-        w1_round = [held([P, 2 * P * PACK], BF16, ("w1_round0", "w1_round1", "w1_round2", "page2")[n]) for n in range(4)]
+        w1_round = [held([P, 2 * P * PACK], BF16, ("w1_round0", "page2", "w1_round2", "page3")[n]) for n in range(4)]
 
         def round_w1(n):
             b, pair = divmod(n, 2)
@@ -164,9 +174,7 @@ def tile_list_bonsai_vigour_rounds_kernel(
 
         def make_features(s):
             b, i = divmod(s, PACK)
-            if s == 1:
-                h = held([P, S], F32, "page3")
-            elif s == SLICES - 1:
+            if s == SLICES - 1:
                 h = held([P, S], F32, "x")
             else:
                 h = ring.tile([P, S], F32, name="h", bufs=3)
@@ -313,22 +321,24 @@ def tile_list_bonsai_vigour_rounds_kernel(
                 nc.sync.dma_start(out[n0 : n0 + P, cols], result[:, 0:width])
 
         x = held([P, PACK, J], F32, "x")
+        deal_w2(0)
         pick_table(0)
         round_w1(0)
         quantize_w1(0)
         pick_table(1)
         make_features(0)
+        deal_w2(1)
         round_w1(1)
         quantize_w1(1)
+        clear_page(2)
         make_features(1)
         round_w1(2)
         round_w1(3)
         quantize_w1(2)
         quantize_w1(3)
-        clear_page(2)
+        clear_page(3)
         make_features(2)
         put(1)
-        clear_page(3)
         make_features(3)
         read(0, x[:, 0, :], 0)
         put(2)
@@ -354,7 +364,7 @@ def tile_list_bonsai_vigour_rounds_kernel(
             add_light(0, x[:, :, first : first + 2 * P], z_round[:, PACK * first : PACK * (first + 2 * P)], first)
         make_features(7)
         put(6)
-        z_words = [held([P, 2, CHUNK], F32, ("w1_round0", "w1_round1", "w1_round2", "w2_raw")[c]) for c in range(J // CHUNK)]
+        z_words = [held([P, 2, CHUNK], F32, ("w1_round0", "table_rows", "w1_round2", "w2_raw")[c]) for c in range(J // CHUNK)]
         for first in range(0, J, BANK):
             add_light_first_pair(x_pair, z_words, first)
         quantize_z(0, z_round[:, 0:2048], 0)

@@ -20,11 +20,15 @@ ALU = mybir.AluOpType
 P = 128
 PACK = 4
 K_PASS = P * PACK
+QUADRANTS = 4
+GROUP = 16
 BANK = 512
 SLICES = H // P
 PAGES = 4
-DIRECT_SLICES = (0, 1, 7)
+DIRECT_SLICES = 2
 CHUNK = 256
+H_BUFFERS = 3
+RESULT_BUFFERS = 3
 
 
 def tile_list_bonsai_vigour_rounds_kernel(
@@ -37,26 +41,21 @@ def tile_list_bonsai_vigour_rounds_kernel(
         ring = ctx.enter_context(tc.tile_pool(name="ring", bufs=2))
         psum = ctx.enter_context(tc.psum_pool(name="psum", bufs=2))
 
-        def held(shape, dtype, name):
-            return keep.tile(shape, dtype, name=name, align_bytes=64)
+        def held(shape, dtype, place):
+            return keep.tile(shape, dtype, name=place, align_bytes=64)
 
-        idx = held([P, S // 16], U16, "idx")
-        idx_put = held([P, S // 16], U16, "idx_put")
-        idx_read = held([P, J // 16], U16, "idx_read")
+        idx = held([P, S // GROUP], U16, "idx")
+        idx_put = held([P, S // GROUP], U16, "idx_put")
+        idx_read = held([P, J // GROUP], U16, "idx_read")
         table = held([P, T], I32, "table")
-        table_scales = held([P, T], U8, "table_scales")
+        table_plane = held([P, T], U8, "table_plane")
         w2_raw = held([P, 2 * H], U8, "w2_raw")
-        w2_raw_scales = held([P, H], U8, "w2_raw_scales")
+        w2_raw_plane = held([P, H], U8, "w2_raw_plane")
         w4_codes = held([P, 2, N], I32, "w4_codes")
         w4_planes = held([P, N], U8, "w4_planes")
-        w1_raw = {}
-
-        def load_w1(b):
-            w1_raw[b] = held([P, PACK, K_PASS], F32, ("w1_raw", "z_round")[b])
-            nc.sync.dma_start(w1_raw[b][:], w1[:, b * K_PASS : (b + 1) * K_PASS].rearrange("(p i) c -> p i c", i=PACK))
-
-        late_raw = [held([P, PACK, N], F32, "late_raw%d" % a) for a in range(3)]
-        light_sb = [held([P, PACK, J], F32, "light%d" % b) for b in range(2)]
+        w1_raw = [held([P, PACK, K_PASS], F32, place) for place in ("w1_raw", "z_round")]
+        score_raw = [held([P, PACK, N], F32, "score_raw%d" % a) for a in range(3)]
+        light_rows = [held([P, PACK, J], F32, "light%d" % b) for b in range(2)]
         bias = held([P, 2, 2 * PACK], F32, "bias")
         gains = held([P, 2, 2 * PACK], F32, "gains")
         put_weight = held([P, S], F32, "put_weight")
@@ -64,224 +63,207 @@ def tile_list_bonsai_vigour_rounds_kernel(
         pages = {n: held([P, T2], F32, "page%d" % n) for n in range(2)}
         identity = held([P, P], F32, "identity")
 
-        def load_scale_rows(rows, name):
-            staged = held([P, rows.shape[1] // 4], I32, name)
-            for q in range(4):
+        def stage_scale_rows(rows, place):
+            staged = held([P, rows.shape[1] // 4], I32, place)
+            for q in range(QUADRANTS):
                 nc.sync.dma_start(staged[32 * q : 32 * q + 4, :], rows[4 * q : 4 * q + 4, :].bitcast(I32))
             return staged
 
         def place_scale_rows(plane, staged):
-            for q in range(4):
+            for q in range(QUADRANTS):
                 nc.vector.tensor_copy(plane[32 * q : 32 * q + 4, :].bitcast(I32), staged[32 * q : 32 * q + 4, :])
 
-        w2_rows = load_scale_rows(w2_scales[0], "w2_rows")
-        table_rows = load_scale_rows(tab_scales[0], "table_rows")
+        def load_rows(tile, rows):
+            nc.sync.dma_start(tile[:], rows.rearrange("(p i) c -> p i c", i=PACK))
+
+        w2_rows = stage_scale_rows(w2_scales[0], "w2_rows")
+        table_rows = stage_scale_rows(tab_scales[0], "table_rows")
         nc.sync.dma_start(w2_raw[:].bitcast(I32), w2_words[0].bitcast(I32))
         nc.sync.dma_start(table[:], tab_words[0].rearrange("p t i -> p (t i)").bitcast(I32))
         nc.sync.dma_start(idx[:], offs)
-        load_w1(0)
+        load_rows(w1_raw[0], w1[:, 0:K_PASS])
         nc.sync.dma_start(bias[:, :, 0:PACK], b1.rearrange("(b p i) -> p b i", b=2, i=PACK))
         nc.sync.dma_start(gains[:, :, 0:PACK], gain.rearrange("(b p i) -> p b i", b=2, i=PACK))
         nc.sync.dma_start(idx_put[:], offs2)
         nc.sync.dma_start(put_weight[:], wgs)
+        load_rows(w1_raw[1], w1[:, K_PASS:H])
         nc.sync.dma_start(idx_read[:], offs3)
         nc.sync.dma_start(read_weight[:], wgt)
-        load_w1(1)
-        nc.sync.dma_start(light_sb[0][:], light[0:K_PASS, :].rearrange("(p i) j -> p i j", i=PACK))
-        late_rows = (w3[0:K_PASS, :], w3[K_PASS:H, :], w5)
-        for a in range(3):
-            nc.sync.dma_start(late_raw[a][:], late_rows[a].rearrange("(p i) n -> p i n", i=PACK))
-        nc.sync.dma_start(light_sb[1][:], light[K_PASS:H, :].rearrange("(p i) j -> p i j", i=PACK))
+        load_rows(light_rows[0], light[0:K_PASS, :])
+        for raw, rows in zip(score_raw, (w3[0:K_PASS, :], w3[K_PASS:H, :], w5)):
+            load_rows(raw, rows)
+        load_rows(light_rows[1], light[K_PASS:H, :])
         nc.sync.dma_start(w4_codes[:], w4_words.rearrange("a p c i -> p a (c i)").bitcast(I32))
-        nc.vector.memset(w4_planes[:].bitcast(I32), 0)
-        for q in range(4):
-            nc.sync.dma_start(w4_planes[32 * q : 32 * q + 8, :].bitcast(I32), w4_scales[:, 4 * q : 4 * q + 4, :].bitcast(I32))
 
-        nc.vector.memset(table_scales[:].bitcast(I32), 0)
-        nc.vector.memset(w2_raw_scales[:].bitcast(I32), 0)
+        nc.vector.memset(table_plane[:].bitcast(I32), 0)
+        nc.vector.memset(w2_raw_plane[:].bitcast(I32), 0)
         for n in range(2):
             nc.vector.memset(pages[n][:], 0.0)
-        place_scale_rows(w2_raw_scales, w2_rows)
-        place_scale_rows(table_scales, table_rows)
+        nc.vector.memset(w4_planes[:].bitcast(I32), 0)
+        for q in range(QUADRANTS):
+            nc.sync.dma_start(w4_planes[32 * q : 32 * q + 8, :].bitcast(I32), w4_scales[:, 4 * q : 4 * q + 4, :].bitcast(I32))
+        place_scale_rows(w2_raw_plane, w2_rows)
+        place_scale_rows(table_plane, table_rows)
         make_identity(nc, identity[:])
 
         w2_codes = held([P, 2 * H], U8, "w2_codes")
         w2_plane = held([P, H], U8, "w2_plane")
-
-        def deal_w2(b):
-            cols = slice(b * K_PASS, (b + 1) * K_PASS)
-            nc.vector.tensor_copy(
-                w2_codes[:].bitcast(U16)[:, cols].rearrange("p (i m) -> p i m", i=PACK),
-                w2_raw[:].bitcast(U16)[:, cols].rearrange("p (m i) -> p i m", i=PACK),
-            )
-            nc.vector.tensor_copy(
-                w2_plane[:, cols].rearrange("p (i m) -> p i m", i=PACK),
-                w2_raw_scales[:, cols].rearrange("p (m i) -> p i m", i=PACK),
-            )
+        nc.vector.tensor_copy(
+            w2_codes[:].bitcast(U16).rearrange("p (b i m) -> p b i m", b=2, i=PACK),
+            w2_raw[:].bitcast(U16).rearrange("p (b m i) -> p b i m", b=2, i=PACK),
+        )
+        nc.vector.tensor_copy(
+            w2_plane[:].rearrange("p (b i m) -> p b i m", b=2, i=PACK),
+            w2_raw_plane[:].rearrange("p (b m i) -> p b i m", b=2, i=PACK),
+        )
 
         v_codes = [held([P, BANK], I32, "v_codes%d" % c) for c in range(2)]
         v_plane = [held([P, BANK], U8, "v_plane%d" % c) for c in range(2)]
 
         def pick_table(c):
-            entries = idx[:, c * BANK // 16 : (c + 1) * BANK // 16]
+            entries = idx[:, c * BANK // GROUP : (c + 1) * BANK // GROUP]
             nc.vector.tensor_copy(v_codes[c][:].bitcast(U32), table[:].bitcast(U32).indirect(entries))
-            nc.vector.tensor_copy(v_plane[c][:], table_scales[:].indirect(entries))
+            nc.vector.tensor_copy(v_plane[c][:], table_plane[:].indirect(entries))
 
-        w1_codes = [held([P, 2 * P], U32, "w1_codes%d" % n) for n in range(4)]
-        w1_plane = [held([P, 2 * P], U8, "w1_plane%d" % n) for n in range(4)]
-        w1_round = [held([P, 2 * P * PACK], BF16, ("w1_round0", "page2", "w1_round2", "page3")[n]) for n in range(4)]
+        w1_codes = held([P, H], U32, "w1_codes")
+        w1_plane = held([P, H], U8, "w1_plane")
 
-        def round_w1(n):
-            b, pair = divmod(n, 2)
+        def prepare_w1(first, count, place):
+            rounded = held([P, count * P * PACK], BF16, place)
+            b, i = divmod(first, PACK)
             nc.scalar.copy(
-                w1_round[n][:].rearrange("p (e m i) -> p m i e", e=2, i=PACK),
-                w1_raw[b][:].rearrange("p i (m t) -> p m i t", t=PACK)[:, :, :, 2 * pair : 2 * pair + 2],
+                rounded[:].rearrange("p (e m k) -> p m k e", e=count, k=PACK),
+                w1_raw[b][:].rearrange("p k (m e) -> p m k e", e=PACK)[:, :, :, i : i + count],
             )
+            cols = slice(first * P, (first + count) * P)
+            nc.vector.quantize_mx(out=w1_codes[:, cols].bitcast(FP8X4), scales=w1_plane[:, cols], in_=rounded[:])
 
-        def quantize_w1(n):
-            nc.vector.quantize_mx(out=w1_codes[n][:].bitcast(FP8X4), scales=w1_plane[n][:], in_=w1_round[n][:])
+        score_round = held([P, 3 * N * PACK], BF16, "score_round")
+        score_codes = held([P, 3 * N], U32, "score_codes")
+        score_plane = held([P, 3 * N], U8, "score_plane")
 
-        late_round = held([P, 3 * N * PACK], BF16, "late_round")
-        late_codes = held([P, 3 * N], U32, "late_codes")
-        late_plane = held([P, 3 * N], U8, "late_plane")
+        def round_score_weights():
+            for a, raw in enumerate(score_raw):
+                nc.scalar.copy(
+                    score_round[:, a * N * PACK : (a + 1) * N * PACK].rearrange("p (c e k) -> p c k e", e=4, k=PACK),
+                    raw[:].rearrange("p k (c e) -> p c k e", e=4),
+                )
 
-        def round_late(a):
-            nc.scalar.copy(
-                late_round[:, a * N * PACK : (a + 1) * N * PACK].rearrange("p (c e i) -> p c i e", e=4, i=PACK),
-                late_raw[a][:].rearrange("p i (c e) -> p c i e", e=4),
-            )
-
-        def quantize_late(first, count):
-            nc.vector.quantize_mx(
-                out=late_codes[:, first : first + count].bitcast(FP8X4),
-                scales=late_plane[:, first : first + count],
-                in_=late_round[:, PACK * first : PACK * (first + count)],
-            )
+        def quantize_score_weights():
+            for first in range(0, 3 * N, BANK):
+                last = min(first + BANK, 3 * N)
+                nc.vector.quantize_mx(
+                    out=score_codes[:, first:last].bitcast(FP8X4),
+                    scales=score_plane[:, first:last],
+                    in_=score_round[:, PACK * first : PACK * last],
+                )
 
         def clear_page(n):
             pages[n] = held([P, T2], F32, "page%d" % n)
             nc.gpsimd.memset(pages[n][:], 0.0)
 
+        def add_transposed(terms):
+            for n, (source, destination) in enumerate(terms):
+                nc.tensor.matmul(
+                    destination, source, identity[:], is_transpose=True, start=(n == 0), stop=(n == len(terms) - 1)
+                )
+
         features = {}
 
-        def put_entries(s, first, count):
+        def put(s, first=0, count=S):
             nc.vector.tensor_tensor(
-                pages[s % PAGES][:].indirect(idx_put[:, first // 16 : (first + count) // 16]),
+                pages[s % PAGES][:].indirect(idx_put[:, first // GROUP : (first + count) // GROUP]),
                 features[s][:, first : first + count],
                 put_weight[:, first : first + count],
                 ALU.mult,
             )
 
-        def make_features(s):
-            b, i = divmod(s, PACK)
-            if s == SLICES - 1:
-                h = held([P, S], F32, "x")
-            else:
-                h = ring.tile([P, S], F32, name="h", bufs=3)
+        def make_features(h, s, c):
             features[s] = h
-            w1_cols = slice((s % 2) * P, (s % 2 + 1) * P)
-            for c in range(2):
-                cols = slice(c * BANK, (c + 1) * BANK)
-                pre = psum.tile([P, BANK], F32, name="sum_a")
-                skip = psum.tile([P, BANK], F32, name="sum_b")
+            b, i = divmod(s, PACK)
+            cols = slice(c * BANK, (c + 1) * BANK)
+            slice_cols = slice(s * P, (s + 1) * P)
+            w2_slice = w2_codes[:, 2 * P * s : 2 * P * (s + 1)].bitcast(FP4X4)
+            pre = psum.tile([P, BANK], F32, name="sum_a")
+            skip = psum.tile([P, BANK], F32, name="sum_b")
+            nc.tensor.matmul_mx(
+                out=pre[:], lhsT=w1_codes[:, slice_cols].bitcast(FP8X4), lhsT_scale=w1_plane[:, slice_cols],
+                rhs=v_codes[c][:].bitcast(FP8X4), rhs_scale=v_plane[c][:], start=True, stop=True,
+            )
+            bent = ring.tile([P, BANK], F32, name="bent")
+            nc.scalar.activation(bent[:], pre[:], ACT.Gelu_apprx_tanh, bias=bias[:, b, i : i + 1])
+            if s < DIRECT_SLICES:
                 nc.tensor.matmul_mx(
-                    out=pre[:], lhsT=w1_codes[s // 2][:, w1_cols].bitcast(FP8X4), lhsT_scale=w1_plane[s // 2][:, w1_cols],
+                    out=skip[:], lhsT=w2_slice, lhsT_scale=w2_plane[:, slice_cols],
                     rhs=v_codes[c][:].bitcast(FP8X4), rhs_scale=v_plane[c][:], start=True, stop=True,
                 )
-                w2_slice = w2_codes[:, 2 * P * s : 2 * P * (s + 1)].bitcast(FP4X4)
-                w2_slice_plane = w2_plane[:, P * s : P * (s + 1)]
-                bent = ring.tile([P, BANK], F32, name="bent")
-                nc.scalar.activation(bent[:], pre[:], ACT.Gelu_apprx_tanh, bias=bias[:, b, i : i + 1])
-                if s in DIRECT_SLICES:
-                    nc.tensor.matmul_mx(
-                        out=skip[:], lhsT=w2_slice, lhsT_scale=w2_slice_plane,
-                        rhs=v_codes[c][:].bitcast(FP8X4), rhs_scale=v_plane[c][:], start=True, stop=True,
-                    )
-                    nc.vector.scalar_tensor_tensor(h[:, cols], bent[:], gains[:, b, i : i + 1], skip[:], ALU.mult, ALU.add)
-                    if s == 0:
-                        put_entries(s, c * BANK, BANK)
-                    continue
-                blocks = [slice(n * P, (n + 1) * P) for n in range(BANK // P)]
-                for block in blocks:
-                    nc.tensor.matmul_mx(
-                        out=skip[:, block], lhsT=v_codes[c][:, block].bitcast(FP8X4), lhsT_scale=v_plane[c][:, block],
-                        rhs=w2_slice, rhs_scale=w2_slice_plane, start=True, stop=True,
-                    )
-                skip_t = ring.tile([P, BANK], F32, name="skip_t")
-                nc.scalar.copy(skip_t[:], skip[:])
-                scaled = ring.tile([P, BANK], F32, name="scaled")
-                nc.scalar.activation(scaled[:], bent[:], ACT.Copy, scale=gains[:, b, i : i + 1])
-                turned = psum.tile([P, BANK], F32, name="turned")
-                for block in blocks:
-                    nc.tensor.transpose(turned[:, block], scaled[:, block], identity[:])
-                scaled_t = ring.tile([P, BANK], F32, name="scaled_t")
-                nc.scalar.copy(scaled_t[:], turned[:])
-                back = psum.tile([P, BANK], F32, name="back")
-                terms = [(term, block) for term in (skip_t, scaled_t) for block in blocks]
-                for n, (term, block) in enumerate(terms):
-                    nc.tensor.matmul(
-                        back[:, block], term[:, block], identity[:], is_transpose=True,
-                        start=(n == 0), stop=(n == len(terms) - 1),
-                    )
-                nc.scalar.copy(h[:, cols], back[:])
+                nc.vector.scalar_tensor_tensor(h[:, cols], bent[:], gains[:, b, i : i + 1], skip[:], ALU.mult, ALU.add)
+                return
+            blocks = [slice(n * P, (n + 1) * P) for n in range(BANK // P)]
+            for block in blocks:
+                nc.tensor.matmul_mx(
+                    out=skip[:, block], lhsT=v_codes[c][:, block].bitcast(FP8X4), lhsT_scale=v_plane[c][:, block],
+                    rhs=w2_slice, rhs_scale=w2_plane[:, slice_cols], start=True, stop=True,
+                )
+            skip_t = ring.tile([P, BANK], F32, name="skip_t")
+            nc.scalar.copy(skip_t[:], skip[:])
+            scaled = ring.tile([P, BANK], F32, name="scaled")
+            nc.scalar.activation(scaled[:], bent[:], ACT.Copy, scale=gains[:, b, i : i + 1])
+            turned = psum.tile([P, BANK], F32, name="turned")
+            for block in blocks:
+                nc.tensor.transpose(turned[:, block], scaled[:, block], identity[:])
+            scaled_t = ring.tile([P, BANK], F32, name="scaled_t")
+            nc.scalar.copy(scaled_t[:], turned[:])
+            back = psum.tile([P, BANK], F32, name="back")
+            add_transposed([(term[:, block], back[:, block]) for term in (skip_t, scaled_t) for block in blocks])
+            nc.scalar.copy(h[:, cols], back[:])
 
-        def put(s):
-            put_entries(s, 0, S)
+        def make_slice(s, place=None):
+            h = held([P, S], F32, place) if place else ring.tile([P, S], F32, name="h", bufs=H_BUFFERS)
+            for c in range(2):
+                make_features(h, s, c)
 
-        def read(s, x_plane, first):
-            width = x_plane.shape[1]
+        def read(s, x, first):
+            width = x.shape[1]
             nc.vector.tensor_tensor(
-                x_plane,
-                pages[s % PAGES][:].indirect(idx_read[:, first // 16 : (first + width) // 16]),
+                x,
+                pages[s % PAGES][:].indirect(idx_read[:, first // GROUP : (first + width) // GROUP]),
                 read_weight[:, first : first + width],
                 ALU.mult,
             )
 
+        def read_pair(s, place):
+            x_pair = held([P, 2, J], F32, place)
+            for e in range(2):
+                read(s + e, x_pair[:, e, :], 0)
+            return x_pair
+
+        def add_light(s, x_pair, words):
+            b, u = s // PACK, s % PACK // 2
+            for first in range(0, J, BANK):
+                back = psum.tile([P, BANK], F32, name="back")
+                for half in range(2):
+                    turned = psum.tile([P, 2, 2, P], F32, name="turned")
+                    start = first + half * 2 * P
+                    add_transposed([
+                        (term[:, e, start + c * P : start + (c + 1) * P], turned[:, c, e, :])
+                        for term in (light_rows[b][:, 2 * u : 2 * u + 2, :], x_pair[:]) for c in range(2) for e in range(2)
+                    ])
+                    pairs = ring.tile([P, 2, P, 2], BF16, name="pairs")
+                    nc.scalar.copy(pairs[:], turned[:].rearrange("j c e p -> j c p e"))
+                    for c in range(2):
+                        column = (2 * half + c) * P
+                        nc.tensor.transpose(
+                            back[:, column : column + P], pairs[:, c].rearrange("j p e -> j (p e)").bitcast(F32), identity[:]
+                        )
+                for half in range(2):
+                    nc.scalar.copy(words[first // CHUNK + half][:, u, :], back[:, half * CHUNK : (half + 1) * CHUNK])
+
+        def weave(z_round, words):
+            nc.scalar.copy(z_round.bitcast(F32).rearrange("p (j u) -> p j u", u=2), words.rearrange("p u j -> p j u"))
+
         z_codes = [held([P, J], U32, "z_codes%d" % b) for b in range(2)]
         z_plane = [held([P, J], U8, "z_plane%d" % b) for b in range(2)]
-
-        def add_light(b, x, z_round, first):
-            back = psum.tile([P, 2, 2, P], F32, name="back")
-            for c in range(2):
-                turned = psum.tile([P, PACK, P], F32, name="turned")
-                terms = [(light_sb[b][:, i, first + c * P : first + (c + 1) * P], i) for i in range(PACK)]
-                terms.extend((x[:, i, c * P : (c + 1) * P], i) for i in range(PACK))
-                for n, (term, i) in enumerate(terms):
-                    nc.tensor.matmul(
-                        turned[:, i, :], term, identity[:], is_transpose=True,
-                        start=(n == 0), stop=(n == len(terms) - 1),
-                    )
-                pairs = ring.tile([P, 2, P, 2], BF16, name="pairs")
-                nc.scalar.copy(pairs[:], turned[:].rearrange("j (u e) p -> j u p e", e=2))
-                for u in range(2):
-                    nc.tensor.transpose(back[:, c, u, :], pairs[:, u].rearrange("j p e -> j (p e)").bitcast(F32), identity[:])
-            nc.scalar.copy(
-                z_round.bitcast(F32).rearrange("p (c j u) -> p c j u", c=2, u=2), back[:].rearrange("p c u j -> p c j u")
-            )
-
-        def add_light_first_pair(x_pair, words, first):
-            back = psum.tile([P, BANK], F32, name="back")
-            for half in range(2):
-                turned = psum.tile([P, 2, 2, P], F32, name="turned")
-                start = first + half * 2 * P
-                terms = [
-                    (term[:, e, start + c * P : start + (c + 1) * P], c, e)
-                    for term in (light_sb[1], x_pair) for c in range(2) for e in range(2)
-                ]
-                for n, (term, c, e) in enumerate(terms):
-                    nc.tensor.matmul(
-                        turned[:, c, e, :], term, identity[:], is_transpose=True,
-                        start=(n == 0), stop=(n == len(terms) - 1),
-                    )
-                pairs = ring.tile([P, 2, P, 2], BF16, name="pairs")
-                nc.scalar.copy(pairs[:], turned[:].rearrange("j c e p -> j c p e"))
-                for c in range(2):
-                    column = (2 * half + c) * P
-                    nc.tensor.transpose(
-                        back[:, column : column + P], pairs[:, c].rearrange("j p e -> j (p e)").bitcast(F32), identity[:]
-                    )
-            for half in range(2):
-                nc.scalar.copy(words[first // CHUNK + half][:, 0, :], back[:, half * CHUNK : (half + 1) * CHUNK])
 
         def quantize_z(b, z_round, first):
             width = z_round.shape[1] // PACK
@@ -291,22 +273,22 @@ def tile_list_bonsai_vigour_rounds_kernel(
                 in_=z_round,
             )
 
-        def score(first, width):
-            cols = slice(first, first + width)
-            half, within = divmod(first, BANK)
-            v_cols = slice(within, within + width)
+        def score(c):
+            cols = slice(c * CHUNK, (c + 1) * CHUNK)
+            half, within = divmod(c * CHUNK, BANK)
+            v_cols = slice(within, within + CHUNK)
             for n0 in range(0, N, P):
-                sums = psum.tile([P, BANK], F32, name=("sum_a", "sum_b", "turned", "back")[(3 * first // width + n0 // P) % 4])
-                stress, rest = sums[:, 0:width], sums[:, width : 2 * width]
+                sums = psum.tile([P, BANK], F32, name=("sum_a", "sum_b", "turned", "back")[(c * N + n0) // P % 4])
+                stress, rest = sums[:, 0:CHUNK], sums[:, CHUNK:BANK]
                 w5_cols = slice(2 * N + n0, 2 * N + n0 + P)
                 nc.tensor.matmul_mx(
-                    out=rest, lhsT=late_codes[:, w5_cols].bitcast(FP8X4), lhsT_scale=late_plane[:, w5_cols],
+                    out=rest, lhsT=score_codes[:, w5_cols].bitcast(FP8X4), lhsT_scale=score_plane[:, w5_cols],
                     rhs=v_codes[half][:, v_cols].bitcast(FP8X4), rhs_scale=v_plane[half][:, v_cols], start=True, stop=False,
                 )
                 for b in range(2):
                     w3_cols = slice(b * N + n0, b * N + n0 + P)
                     nc.tensor.matmul_mx(
-                        out=stress, lhsT=late_codes[:, w3_cols].bitcast(FP8X4), lhsT_scale=late_plane[:, w3_cols],
+                        out=stress, lhsT=score_codes[:, w3_cols].bitcast(FP8X4), lhsT_scale=score_plane[:, w3_cols],
                         rhs=z_codes[b][:, cols].bitcast(FP8X4), rhs_scale=z_plane[b][:, cols], start=False, stop=False,
                     )
                     nc.tensor.matmul_mx(
@@ -314,74 +296,65 @@ def tile_list_bonsai_vigour_rounds_kernel(
                         lhsT_scale=w4_planes[4 * b : P, n0 : n0 + P],
                         rhs=z_codes[b][:, cols].bitcast(FP8X4), rhs_scale=z_plane[b][:, cols], start=False, stop=(b == 1),
                     )
-                size = ring.tile([P, width], F32, name="size")
-                nc.scalar.activation(size[:, 0:width], stress, ACT.Abs)
-                result = ring.tile([P, width], F32, name="result", bufs=3)
-                nc.vector.tensor_tensor(result[:, 0:width], size[:, 0:width], rest, ALU.add)
-                nc.sync.dma_start(out[n0 : n0 + P, cols], result[:, 0:width])
+                size = ring.tile([P, CHUNK], F32, name="size")
+                nc.scalar.activation(size[:], stress, ACT.Abs)
+                result = ring.tile([P, CHUNK], F32, name="result", bufs=RESULT_BUFFERS)
+                nc.vector.tensor_tensor(result[:], size[:], rest, ALU.add)
+                nc.sync.dma_start(out[n0 : n0 + P, cols], result[:])
 
-        x = held([P, PACK, J], F32, "x")
-        deal_w2(0)
         pick_table(0)
-        round_w1(0)
-        quantize_w1(0)
+        prepare_w1(0, 2, "w1_round")
         pick_table(1)
-        make_features(0)
-        deal_w2(1)
-        round_w1(1)
-        quantize_w1(1)
+        h_first = ring.tile([P, S], F32, name="h", bufs=H_BUFFERS)
+        for c in range(2):
+            make_features(h_first, 0, c)
+            put(0, c * BANK, BANK)
+        prepare_w1(2, 2, "page2")
         clear_page(2)
-        make_features(1)
-        round_w1(2)
-        round_w1(3)
-        quantize_w1(2)
-        quantize_w1(3)
-        clear_page(3)
-        make_features(2)
+        prepare_w1(4, 4, "page3")
+        make_slice(1, "page3")
+        make_slice(2)
         put(1)
-        make_features(3)
-        read(0, x[:, 0, :], 0)
+        clear_page(3)
+
+        make_slice(3)
+        round_score_weights()
+        low_words = held([P, 2, J], F32, "w1_raw")
+        low_chunks = [low_words[:, :, c * CHUNK : (c + 1) * CHUNK] for c in range(J // CHUNK)]
+        add_light(0, read_pair(0, "x_even"), low_chunks)
         put(2)
-        make_features(4)
-        for a in range(3):
-            round_late(a)
-        read(1, x[:, 1, :], 0)
+        make_slice(4)
         put(3)
-        make_features(5)
-        read(2, x[:, 2, :], 0)
-        read(3, x[:, 3, :], 0)
-        put(4)
-        make_features(6)
-        quantize_late(0, 512)
-        quantize_late(512, 512)
-        quantize_late(1024, 128)
-        put(5)
+        quantize_score_weights()
+        make_slice(5)
+        add_light(2, read_pair(2, "x_odd"), low_chunks)
         z_round = held([P, J * PACK], BF16, "z_round")
-        x_pair = held([P, 2, J], F32, "table")
-        read(4, x_pair[:, 0, :], 0)
-        read(5, x_pair[:, 1, :], 0)
-        for first in range(0, J, 2 * P):
-            add_light(0, x[:, :, first : first + 2 * P], z_round[:, PACK * first : PACK * (first + 2 * P)], first)
-        make_features(7)
-        put(6)
-        z_words = [held([P, 2, CHUNK], F32, ("w1_round0", "table_rows", "w1_round2", "w2_raw")[c]) for c in range(J // CHUNK)]
         for first in range(0, J, BANK):
-            add_light_first_pair(x_pair, z_words, first)
-        quantize_z(0, z_round[:, 0:2048], 0)
-        quantize_z(0, z_round[:, 2048:4096], 512)
+            weave(z_round[:, PACK * first : PACK * (first + BANK)], low_words[:, :, first : first + BANK])
+
+        put(4)
+        make_slice(6)
+        put(5)
+        x_pair = read_pair(4, "x_even")
+        for first in range(0, J, BANK):
+            quantize_z(0, z_round[:, PACK * first : PACK * (first + BANK)], first)
+        make_slice(7, "x_odd")
+        put(6)
+        high_words = [held([P, 2, CHUNK], F32, place) for place in ("w1_round", "table_rows", "w2_rows", "w2_raw")]
+        add_light(4, x_pair, high_words)
         put(7)
-        x_last = held([P, J // CHUNK, 2, CHUNK], F32, "x")
+
+        x_last = held([P, J // CHUNK, 2, CHUNK], F32, "x_odd")
         for c in range(J // CHUNK):
-            cols = slice(c * CHUNK, (c + 1) * CHUNK)
             for e in range(2):
-                read(6 + e, x_last[:, c, e, :], c * CHUNK)
+                read(SLICES - 2 + e, x_last[:, c, e, :], c * CHUNK)
             nc.vector.tensor_tensor(
-                z_words[c][:, 1, :].bitcast(BF16).rearrange("p (j e) -> p j e", e=2),
+                high_words[c][:, 1, :].bitcast(BF16).rearrange("p (j e) -> p j e", e=2),
                 x_last[:, c].rearrange("p e j -> p j e"),
-                light_sb[1][:, 2:4, cols].rearrange("p e j -> p j e"),
+                light_rows[1][:, 2:PACK, c * CHUNK : (c + 1) * CHUNK].rearrange("p e j -> p j e"),
                 ALU.add,
             )
             z_chunk = ring.tile([P, CHUNK * PACK], BF16, name="z_chunk", align_bytes=64)
-            nc.scalar.copy(z_chunk[:].bitcast(F32).rearrange("p (j u) -> p j u", u=2), z_words[c][:].rearrange("p u j -> p j u"))
+            weave(z_chunk[:], high_words[c][:])
             quantize_z(1, z_chunk[:], c * CHUNK)
-            score(c * CHUNK, CHUNK)
+            score(c)

from contextlib import ExitStack

import concourse.mybir as mybir
from concourse.masks import make_identity

K, T, S, H, T2, J, N = 512, 4096, 1024, 1024, 2048, 1024, 384
FLOPS = 2 * (2 * K * H * S + 2 * H * N * J + K * N * S)

F32 = mybir.dt.float32
BF16 = mybir.dt.bfloat16
I32 = mybir.dt.int32
U32 = mybir.dt.uint32
U16 = mybir.dt.uint16
U8 = mybir.dt.uint8
FP8X4 = mybir.dt.float8_e4m3fn_x4
FP4X4 = mybir.dt.float4_e2m1fn_x4
ACT = mybir.ActivationFunctionType
ALU = mybir.AluOpType

P = 128
PACK = 4
K_PASS = P * PACK
QUADRANTS = 4
GROUP = 16
BANK = 512
SLICES = H // P
PAGES = 4
DIRECT_SLICES = 2
CHUNK = 256
H_BUFFERS = 3
RESULT_BUFFERS = 3


def tile_list_bonsai_vigour_rounds_kernel(
    tc, tab_words, tab_scales, offs, offs2, offs3, w1, b1, gain, w2_words, w2_scales,
    wgs, wgt, light, w3, w4_words, w4_scales, w5, out,
):
    nc = tc.nc
    with ExitStack() as ctx:
        keep = ctx.enter_context(tc.tile_pool(name="keep", bufs=1))
        ring = ctx.enter_context(tc.tile_pool(name="ring", bufs=2))
        psum = ctx.enter_context(tc.psum_pool(name="psum", bufs=2))

        def held(shape, dtype, place):
            return keep.tile(shape, dtype, name=place, align_bytes=64)

        idx = held([P, S // GROUP], U16, "idx")
        idx_put = held([P, S // GROUP], U16, "idx_put")
        idx_read = held([P, J // GROUP], U16, "idx_read")
        table = held([P, T], I32, "table")
        table_plane = held([P, T], U8, "table_plane")
        w2_raw = held([P, 2 * H], U8, "w2_raw")
        w2_raw_plane = held([P, H], U8, "w2_raw_plane")
        w4_codes = held([P, 2, N], I32, "w4_codes")
        w4_planes = held([P, N], U8, "w4_planes")
        w1_raw = [held([P, PACK, K_PASS], F32, place) for place in ("w1_raw", "z_round")]
        score_raw = [held([P, PACK, N], F32, "score_raw%d" % a) for a in range(3)]
        light_rows = [held([P, PACK, J], F32, "light%d" % b) for b in range(2)]
        bias = held([P, 2, 2 * PACK], F32, "bias")
        gains = held([P, 2, 2 * PACK], F32, "gains")
        put_weight = held([P, S], F32, "put_weight")
        read_weight = held([P, J], F32, "read_weight")
        pages = {n: held([P, T2], F32, "page%d" % n) for n in range(2)}
        identity = held([P, P], F32, "identity")

        def stage_scale_rows(rows, place):
            staged = held([P, rows.shape[1] // 4], I32, place)
            for q in range(QUADRANTS):
                nc.sync.dma_start(staged[32 * q : 32 * q + 4, :], rows[4 * q : 4 * q + 4, :].bitcast(I32))
            return staged

        def place_scale_rows(plane, staged):
            for q in range(QUADRANTS):
                nc.vector.tensor_copy(plane[32 * q : 32 * q + 4, :].bitcast(I32), staged[32 * q : 32 * q + 4, :])

        def load_rows(tile, rows):
            nc.sync.dma_start(tile[:], rows.rearrange("(p i) c -> p i c", i=PACK))

        w2_rows = stage_scale_rows(w2_scales[0], "w2_rows")
        table_rows = stage_scale_rows(tab_scales[0], "table_rows")
        nc.sync.dma_start(w2_raw[:].bitcast(I32), w2_words[0].bitcast(I32))
        nc.sync.dma_start(table[:], tab_words[0].rearrange("p t i -> p (t i)").bitcast(I32))
        nc.sync.dma_start(idx[:], offs)
        load_rows(w1_raw[0], w1[:, 0:K_PASS])
        nc.sync.dma_start(bias[:, :, 0:PACK], b1.rearrange("(b p i) -> p b i", b=2, i=PACK))
        nc.sync.dma_start(gains[:, :, 0:PACK], gain.rearrange("(b p i) -> p b i", b=2, i=PACK))
        nc.sync.dma_start(idx_put[:], offs2)
        nc.sync.dma_start(put_weight[:], wgs)
        load_rows(w1_raw[1], w1[:, K_PASS:H])
        nc.sync.dma_start(idx_read[:], offs3)
        nc.sync.dma_start(read_weight[:], wgt)
        load_rows(light_rows[0], light[0:K_PASS, :])
        for raw, rows in zip(score_raw, (w3[0:K_PASS, :], w3[K_PASS:H, :], w5)):
            load_rows(raw, rows)
        load_rows(light_rows[1], light[K_PASS:H, :])
        nc.sync.dma_start(w4_codes[:], w4_words.rearrange("a p c i -> p a (c i)").bitcast(I32))

        nc.vector.memset(table_plane[:].bitcast(I32), 0)
        nc.vector.memset(w2_raw_plane[:].bitcast(I32), 0)
        for n in range(2):
            nc.vector.memset(pages[n][:], 0.0)
        nc.vector.memset(w4_planes[:].bitcast(I32), 0)
        for q in range(QUADRANTS):
            nc.sync.dma_start(w4_planes[32 * q : 32 * q + 8, :].bitcast(I32), w4_scales[:, 4 * q : 4 * q + 4, :].bitcast(I32))
        place_scale_rows(w2_raw_plane, w2_rows)
        place_scale_rows(table_plane, table_rows)
        make_identity(nc, identity[:])

        w2_codes = held([P, 2 * H], U8, "w2_codes")
        w2_plane = held([P, H], U8, "w2_plane")
        nc.vector.tensor_copy(
            w2_codes[:].bitcast(U16).rearrange("p (b i m) -> p b i m", b=2, i=PACK),
            w2_raw[:].bitcast(U16).rearrange("p (b m i) -> p b i m", b=2, i=PACK),
        )
        nc.vector.tensor_copy(
            w2_plane[:].rearrange("p (b i m) -> p b i m", b=2, i=PACK),
            w2_raw_plane[:].rearrange("p (b m i) -> p b i m", b=2, i=PACK),
        )

        v_codes = [held([P, BANK], I32, "v_codes%d" % c) for c in range(2)]
        v_plane = [held([P, BANK], U8, "v_plane%d" % c) for c in range(2)]

        def pick_table(c):
            entries = idx[:, c * BANK // GROUP : (c + 1) * BANK // GROUP]
            nc.vector.tensor_copy(v_codes[c][:].bitcast(U32), table[:].bitcast(U32).indirect(entries))
            nc.vector.tensor_copy(v_plane[c][:], table_plane[:].indirect(entries))

        w1_codes = held([P, H], U32, "w1_codes")
        w1_plane = held([P, H], U8, "w1_plane")

        def prepare_w1(first, count, place):
            rounded = held([P, count * P * PACK], BF16, place)
            b, i = divmod(first, PACK)
            nc.scalar.copy(
                rounded[:].rearrange("p (e m k) -> p m k e", e=count, k=PACK),
                w1_raw[b][:].rearrange("p k (m e) -> p m k e", e=PACK)[:, :, :, i : i + count],
            )
            cols = slice(first * P, (first + count) * P)
            nc.vector.quantize_mx(out=w1_codes[:, cols].bitcast(FP8X4), scales=w1_plane[:, cols], in_=rounded[:])

        score_round = held([P, 3 * N * PACK], BF16, "score_round")
        score_codes = held([P, 3 * N], U32, "score_codes")
        score_plane = held([P, 3 * N], U8, "score_plane")

        def round_score_weights():
            for a, raw in enumerate(score_raw):
                nc.scalar.copy(
                    score_round[:, a * N * PACK : (a + 1) * N * PACK].rearrange("p (c e k) -> p c k e", e=4, k=PACK),
                    raw[:].rearrange("p k (c e) -> p c k e", e=4),
                )

        def quantize_score_weights():
            for first in range(0, 3 * N, BANK):
                last = min(first + BANK, 3 * N)
                nc.vector.quantize_mx(
                    out=score_codes[:, first:last].bitcast(FP8X4),
                    scales=score_plane[:, first:last],
                    in_=score_round[:, PACK * first : PACK * last],
                )

        def clear_page(n):
            pages[n] = held([P, T2], F32, "page%d" % n)
            nc.gpsimd.memset(pages[n][:], 0.0)

        def add_transposed(terms):
            for n, (source, destination) in enumerate(terms):
                nc.tensor.matmul(
                    destination, source, identity[:], is_transpose=True, start=(n == 0), stop=(n == len(terms) - 1)
                )

        features = {}

        def put(s, first=0, count=S):
            nc.vector.tensor_tensor(
                pages[s % PAGES][:].indirect(idx_put[:, first // GROUP : (first + count) // GROUP]),
                features[s][:, first : first + count],
                put_weight[:, first : first + count],
                ALU.mult,
            )

        def make_features(h, s, c):
            features[s] = h
            b, i = divmod(s, PACK)
            cols = slice(c * BANK, (c + 1) * BANK)
            slice_cols = slice(s * P, (s + 1) * P)
            w2_slice = w2_codes[:, 2 * P * s : 2 * P * (s + 1)].bitcast(FP4X4)
            pre = psum.tile([P, BANK], F32, name="sum_a")
            skip = psum.tile([P, BANK], F32, name="sum_b")
            nc.tensor.matmul_mx(
                out=pre[:], lhsT=w1_codes[:, slice_cols].bitcast(FP8X4), lhsT_scale=w1_plane[:, slice_cols],
                rhs=v_codes[c][:].bitcast(FP8X4), rhs_scale=v_plane[c][:], start=True, stop=True,
            )
            bent = ring.tile([P, BANK], F32, name="bent")
            nc.scalar.activation(bent[:], pre[:], ACT.Gelu_apprx_tanh, bias=bias[:, b, i : i + 1])
            if s < DIRECT_SLICES:
                nc.tensor.matmul_mx(
                    out=skip[:], lhsT=w2_slice, lhsT_scale=w2_plane[:, slice_cols],
                    rhs=v_codes[c][:].bitcast(FP8X4), rhs_scale=v_plane[c][:], start=True, stop=True,
                )
                nc.vector.scalar_tensor_tensor(h[:, cols], bent[:], gains[:, b, i : i + 1], skip[:], ALU.mult, ALU.add)
                return
            blocks = [slice(n * P, (n + 1) * P) for n in range(BANK // P)]
            for block in blocks:
                nc.tensor.matmul_mx(
                    out=skip[:, block], lhsT=v_codes[c][:, block].bitcast(FP8X4), lhsT_scale=v_plane[c][:, block],
                    rhs=w2_slice, rhs_scale=w2_plane[:, slice_cols], start=True, stop=True,
                )
            skip_t = ring.tile([P, BANK], F32, name="skip_t")
            nc.scalar.copy(skip_t[:], skip[:])
            scaled = ring.tile([P, BANK], F32, name="scaled")
            nc.scalar.activation(scaled[:], bent[:], ACT.Copy, scale=gains[:, b, i : i + 1])
            turned = psum.tile([P, BANK], F32, name="turned")
            for block in blocks:
                nc.tensor.transpose(turned[:, block], scaled[:, block], identity[:])
            scaled_t = ring.tile([P, BANK], F32, name="scaled_t")
            nc.scalar.copy(scaled_t[:], turned[:])
            back = psum.tile([P, BANK], F32, name="back")
            add_transposed([(term[:, block], back[:, block]) for term in (skip_t, scaled_t) for block in blocks])
            nc.scalar.copy(h[:, cols], back[:])

        def make_slice(s, place=None):
            h = held([P, S], F32, place) if place else ring.tile([P, S], F32, name="h", bufs=H_BUFFERS)
            for c in range(2):
                make_features(h, s, c)

        def read(s, x, first):
            width = x.shape[1]
            nc.vector.tensor_tensor(
                x,
                pages[s % PAGES][:].indirect(idx_read[:, first // GROUP : (first + width) // GROUP]),
                read_weight[:, first : first + width],
                ALU.mult,
            )

        def read_pair(s, place):
            x_pair = held([P, 2, J], F32, place)
            for e in range(2):
                read(s + e, x_pair[:, e, :], 0)
            return x_pair

        def add_light(s, x_pair, words):
            b, u = s // PACK, s % PACK // 2
            for first in range(0, J, BANK):
                back = psum.tile([P, BANK], F32, name="back")
                for half in range(2):
                    turned = psum.tile([P, 2, 2, P], F32, name="turned")
                    start = first + half * 2 * P
                    add_transposed([
                        (term[:, e, start + c * P : start + (c + 1) * P], turned[:, c, e, :])
                        for term in (light_rows[b][:, 2 * u : 2 * u + 2, :], x_pair[:]) for c in range(2) for e in range(2)
                    ])
                    pairs = ring.tile([P, 2, P, 2], BF16, name="pairs")
                    nc.scalar.copy(pairs[:], turned[:].rearrange("j c e p -> j c p e"))
                    for c in range(2):
                        column = (2 * half + c) * P
                        nc.tensor.transpose(
                            back[:, column : column + P], pairs[:, c].rearrange("j p e -> j (p e)").bitcast(F32), identity[:]
                        )
                for half in range(2):
                    nc.scalar.copy(words[first // CHUNK + half][:, u, :], back[:, half * CHUNK : (half + 1) * CHUNK])

        def weave(z_round, words):
            nc.scalar.copy(z_round.bitcast(F32).rearrange("p (j u) -> p j u", u=2), words.rearrange("p u j -> p j u"))

        z_codes = [held([P, J], U32, "z_codes%d" % b) for b in range(2)]
        z_plane = [held([P, J], U8, "z_plane%d" % b) for b in range(2)]

        def quantize_z(b, z_round, first):
            width = z_round.shape[1] // PACK
            nc.vector.quantize_mx(
                out=z_codes[b][:, first : first + width].bitcast(FP8X4),
                scales=z_plane[b][:, first : first + width],
                in_=z_round,
            )

        def score(c):
            cols = slice(c * CHUNK, (c + 1) * CHUNK)
            half, within = divmod(c * CHUNK, BANK)
            v_cols = slice(within, within + CHUNK)
            for n0 in range(0, N, P):
                sums = psum.tile([P, BANK], F32, name=("sum_a", "sum_b", "turned", "back")[(c * N + n0) // P % 4])
                stress, rest = sums[:, 0:CHUNK], sums[:, CHUNK:BANK]
                w5_cols = slice(2 * N + n0, 2 * N + n0 + P)
                nc.tensor.matmul_mx(
                    out=rest, lhsT=score_codes[:, w5_cols].bitcast(FP8X4), lhsT_scale=score_plane[:, w5_cols],
                    rhs=v_codes[half][:, v_cols].bitcast(FP8X4), rhs_scale=v_plane[half][:, v_cols], start=True, stop=False,
                )
                for b in range(2):
                    w3_cols = slice(b * N + n0, b * N + n0 + P)
                    nc.tensor.matmul_mx(
                        out=stress, lhsT=score_codes[:, w3_cols].bitcast(FP8X4), lhsT_scale=score_plane[:, w3_cols],
                        rhs=z_codes[b][:, cols].bitcast(FP8X4), rhs_scale=z_plane[b][:, cols], start=False, stop=False,
                    )
                    nc.tensor.matmul_mx(
                        out=rest, lhsT=w4_codes[:, b, n0 : n0 + P].bitcast(FP8X4),
                        lhsT_scale=w4_planes[4 * b : P, n0 : n0 + P],
                        rhs=z_codes[b][:, cols].bitcast(FP8X4), rhs_scale=z_plane[b][:, cols], start=False, stop=(b == 1),
                    )
                size = ring.tile([P, CHUNK], F32, name="size")
                nc.scalar.activation(size[:], stress, ACT.Abs)
                result = ring.tile([P, CHUNK], F32, name="result", bufs=RESULT_BUFFERS)
                nc.vector.tensor_tensor(result[:], size[:], rest, ALU.add)
                nc.sync.dma_start(out[n0 : n0 + P, cols], result[:])

        pick_table(0)
        prepare_w1(0, 2, "w1_round")
        pick_table(1)
        h_first = ring.tile([P, S], F32, name="h", bufs=H_BUFFERS)
        for c in range(2):
            make_features(h_first, 0, c)
            put(0, c * BANK, BANK)
        prepare_w1(2, 2, "page2")
        clear_page(2)
        prepare_w1(4, 4, "page3")
        make_slice(1, "page3")
        make_slice(2)
        put(1)
        clear_page(3)

        make_slice(3)
        round_score_weights()
        low_words = held([P, 2, J], F32, "w1_raw")
        low_chunks = [low_words[:, :, c * CHUNK : (c + 1) * CHUNK] for c in range(J // CHUNK)]
        add_light(0, read_pair(0, "x_even"), low_chunks)
        put(2)
        make_slice(4)
        put(3)
        quantize_score_weights()
        make_slice(5)
        add_light(2, read_pair(2, "x_odd"), low_chunks)
        z_round = held([P, J * PACK], BF16, "z_round")
        for first in range(0, J, BANK):
            weave(z_round[:, PACK * first : PACK * (first + BANK)], low_words[:, :, first : first + BANK])

        put(4)
        make_slice(6)
        put(5)
        x_pair = read_pair(4, "x_even")
        for first in range(0, J, BANK):
            quantize_z(0, z_round[:, PACK * first : PACK * (first + BANK)], first)
        make_slice(7, "x_odd")
        put(6)
        high_words = [held([P, 2, CHUNK], F32, place) for place in ("w1_round", "table_rows", "w2_rows", "w2_raw")]
        add_light(4, x_pair, high_words)
        put(7)

        x_last = held([P, J // CHUNK, 2, CHUNK], F32, "x_odd")
        for c in range(J // CHUNK):
            for e in range(2):
                read(SLICES - 2 + e, x_last[:, c, e, :], c * CHUNK)
            nc.vector.tensor_tensor(
                high_words[c][:, 1, :].bitcast(BF16).rearrange("p (j e) -> p j e", e=2),
                x_last[:, c].rearrange("p e j -> p j e"),
                light_rows[1][:, 2:PACK, c * CHUNK : (c + 1) * CHUNK].rearrange("p e j -> p j e"),
                ALU.add,
            )
            z_chunk = ring.tile([P, CHUNK * PACK], BF16, name="z_chunk", align_bytes=64)
            weave(z_chunk[:], high_words[c][:])
            quantize_z(1, z_chunk[:], c * CHUNK)
            score(c)
